import numpy as np
import ml_dtypes


def mxq(x, axis, fmt="e4m3"):
    dtype, down = {"e4m3": (ml_dtypes.float8_e4m3fn, 7), "e5m2": (ml_dtypes.float8_e5m2, 14)}[fmt]
    v = np.moveaxis(np.asarray(x, np.float32).astype(ml_dtypes.bfloat16).astype(np.float64), axis, -1)
    blocks = v.reshape(v.shape[:-1] + (-1, 32))
    amax = np.abs(blocks).max(-1, keepdims=True)
    byte = np.maximum(np.where(amax > 0, np.frexp(amax)[1] - 1 + 127, 0) - down, 1)
    scale = np.exp2(byte - 127.0)
    codes = (blocks / scale).astype(np.float32).astype(dtype).astype(np.float64)
    return np.moveaxis((codes * scale).reshape(v.shape), -1, axis)


WIDE = False


def mx_kscale(k):
    if not WIDE:
        return np.ones(k)
    levels = np.array([10, -10, 5, -5, 0])
    if k % 512:
        return np.exp2(np.random.permutation(np.resize(levels, k // 32))).repeat(32)
    a = np.empty((k // 512, 16))
    for p in range(k // 512):
        a[p, :8] = np.random.permutation(np.resize(levels, 8))
        for g in range(8):
            far = levels[np.abs(levels - a[p, g]) >= 10]
            a[p, g + 8] = far[np.random.randint(len(far))]
    return np.exp2(a.ravel()).repeat(32)


def f64(x):
    return np.asarray(x).astype(np.float64)


def striped(idx):
    return np.tile(idx.reshape(-1, 16).T, (8, 1)).astype(np.uint16)


def unstriped(offs):
    return offs[:16].T.reshape(-1).astype(np.int64)


def striped8(idx):
    return np.concatenate([x.reshape(-1, 16).T for x in idx]).astype(np.uint16)


def runs(offs, k):
    lists = np.stack([offs[16 * r : 16 * r + 16].T.reshape(-1) for r in range(8)]).astype(np.int64)
    return lists[np.arange(k) % 512 // 64]


def pack_weight(w):
    k, n = w.shape
    w = f64(np.asarray(w, np.float32).astype(ml_dtypes.bfloat16)).reshape(k // 32, 32, n)
    amax = np.abs(w).max(1)
    byte = np.clip(np.where(amax > 0, np.frexp(amax)[1] - 1 + 127 - 7, 1), 1, 254)
    scaled = (w * np.exp2(127.0 - byte)[:, None, :]).reshape(k, n).astype(np.float32)
    words = np.ascontiguousarray(scaled.reshape(k // 512, 128, 4, n).transpose(0, 1, 3, 2)).astype(ml_dtypes.float8_e4m3fn).view(np.uint8)
    return words, np.ascontiguousarray(byte.astype(np.uint8).reshape(k // 512, 16, n))


def unpack_weight(words, scales):
    g, p, n, _ = words.shape
    vals = np.ascontiguousarray(words).view(ml_dtypes.float8_e4m3fn).astype(np.float64) * np.repeat(np.exp2(scales.astype(np.float64) - 127.0), 8, axis=1)[..., None]
    return vals.transpose(0, 1, 3, 2).reshape(g * 512, n)


E2M1 = np.array([0.0, 0.5, 1.0, 1.5, 2.0, 3.0, 4.0, 6.0, -0.0, -0.5, -1.0, -1.5, -2.0, -3.0, -4.0, -6.0])


def pack_fp4(w):
    k, n = w.shape
    w = f64(np.asarray(w, np.float32).astype(ml_dtypes.bfloat16)).reshape(k // 32, 32, n)
    amax = np.abs(w).max(1)
    mant, ex = np.frexp(amax / 6.0)
    byte = np.clip(np.where(amax > 0, np.where(mant > 0.5, ex, ex - 1) + 127, 1), 1, 254)
    scaled = (w * np.exp2(127.0 - byte)[:, None, :]).reshape(k, n).astype(np.float32)
    c = np.ascontiguousarray(scaled.reshape(k // 512, 128, 4, n).transpose(0, 1, 3, 2)).astype(ml_dtypes.float4_e2m1fn).view(np.uint8) & 0xF
    words = (c[..., 0::2] | (c[..., 1::2] << 4)).reshape(k // 512, 128, 2 * n)
    return np.ascontiguousarray(words), np.ascontiguousarray(byte.astype(np.uint8).reshape(k // 512, 16, n))


def unpack_fp4(words, scales):
    g, _, n = scales.shape
    words = np.ascontiguousarray(words).reshape(g, 128, n, 2)
    nib = np.empty((g, 128, n, 4), np.uint8)
    nib[..., 0::2] = words & 0xF
    nib[..., 1::2] = words >> 4
    vals = E2M1[nib] * np.repeat(np.exp2(scales.astype(np.float64) - 127.0), 8, axis=1)[..., None]
    return vals.transpose(0, 1, 3, 2).reshape(g * 512, n)


def relu(v):
    return np.maximum(v, 0.0)


K, T, S, H, N, V = 512, 2048, 1024, 512, 256, 512


def setup_inputs():
    n = np.random.standard_normal
    s = mx_kscale(K)[:, None]
    u = mx_kscale(H)
    packed_xT = pack_weight(n((K, T)) * s)
    packed_w2 = pack_fp4(n((H, N)) / np.sqrt(H) / u[:, None])
    return {
        "x_words": packed_xT[0],
        "x_scales": packed_xT[1],
        "w1": (n((K, H)) / np.sqrt(K) / s * u).astype(np.float32),
        "w2_words": packed_w2[0],
        "w2_scales": packed_w2[1],
        "offs": striped8(np.stack([np.random.permutation(T)[:S] for _ in range(8)])),
        "left": striped(np.random.permutation(S)[:V]),
        "right": striped(np.random.permutation(S)[:V]),
    }


def reference(x_words, x_scales, w1, w2_words, w2_scales, offs, left, right):
    xq = unpack_weight(x_words, x_scales)[np.arange(K)[:, None], runs(offs, K)]
    h = mxq(f64(w1), 0, "e4m3").T @ xq
    z = relu(h[:, unstriped(left)] - h[:, unstriped(right)])
    return unpack_fp4(w2_words, w2_scales).T @ mxq(z, 0, "e4m3")

@@ -1,0 +1,213 @@
+from contextlib import ExitStack
+
+import concourse.mybir as mybir
+
+K, T, S, H, N, V = 512, 2048, 1024, 512, 256, 512
+FLOPS = 2 * K * H * S + 2 * H * N * V
+
+F32 = mybir.dt.float32
+BF16 = mybir.dt.bfloat16
+I32 = mybir.dt.int32
+U32 = mybir.dt.uint32
+U16 = mybir.dt.uint16
+U8 = mybir.dt.uint8
+FP8X4 = mybir.dt.float8_e4m3fn_x4
+FP4X4 = mybir.dt.float4_e2m1fn_x4
+ALU = mybir.AluOpType
+ACT = mybir.ActivationFunctionType
+
+P = 128
+PACK = 4
+PIECE = 256
+PAIR_CHUNKS = (256, 128, 128)
+
+
+def tile_picked_phpair_relu_p_kernel(
+    tc, x_words, x_scales, w1, w2_words, w2_scales, offs, left, right, out
+):
+    nc = tc.nc
+    with ExitStack() as ctx:
+        lists = ctx.enter_context(tc.tile_pool(name="lists", bufs=1))
+        keep = ctx.enter_context(tc.tile_pool(name="keep", bufs=1))
+        h_psum = ctx.enter_context(tc.psum_pool(name="h_psum", bufs=6))
+        o_psum = ctx.enter_context(tc.psum_pool(name="o_psum", bufs=2))
+
+        offs_sb = lists.tile([P, S // 16], U16, name="offs_sb")
+        left_sb = lists.tile([P, V // 16], U16, name="left_sb")
+        right_sb = lists.tile([P, V // 16], U16, name="right_sb")
+
+        xs_table = keep.tile([P, T], U8, name="xs_table", align_bytes=64)
+        xs_picked = keep.tile([P, S], U8, name="xs_picked", align_bytes=64)
+        xs_plane = keep.tile([P, S], U8, name="xs_plane", align_bytes=64)
+        xw_table = keep.tile([P, T], U32, name="xw_table", align_bytes=64)
+        w1_raw = [keep.tile([P, PACK, H // 2], F32, name="w1_raw%d" % a, align_bytes=64) for a in range(2)]
+        w1_bf = keep.tile([P, PACK * H], BF16, name="w1_bf", align_bytes=64)
+        w1_codes = keep.tile([P, H], U32, name="w1_codes", align_bytes=64)
+        w1_plane = keep.tile([P, H], U8, name="w1_plane", align_bytes=64)
+        w2_codes = keep.tile([P, 2 * N], U8, name="w2_codes", align_bytes=64)
+        w2_plane = keep.tile([P, N], U8, name="w2_plane", align_bytes=64)
+
+        warm = keep.tile([P, 16], F32, name="warm", align_bytes=64)
+        nc.vector.memset(warm[:, 0:8], 0.0)
+        nc.scalar.activation(out=warm[:, 8:16], in_=warm[:, 0:8], func=ACT.Relu)
+        nc.vector.memset(xs_plane[:].bitcast(I32), 0)
+        nc.vector.memset(w2_plane[:].bitcast(I32), 0)
+
+        nc.sync.dma_start(offs_sb[:], offs)
+        nc.sync.dma_start(
+            out=xs_table[:].bitcast(I32),
+            in_=x_scales[0].bitcast(I32).unsqueeze(1).broadcast_to([16, 8, T // 4]),
+        )
+        nc.sync.dma_start(
+            out=xw_table[:].bitcast(I32), in_=x_words[0].rearrange("p c r -> p (c r)").bitcast(I32)
+        )
+        w1_rows = w1.rearrange("(p j) c -> p j c", j=PACK)
+        for a in range(2):
+            nc.sync.dma_start(out=w1_raw[a][:], in_=w1_rows[:, :, 256 * a : 256 * (a + 1)])
+        nc.sync.dma_start(left_sb[:], left)
+        nc.sync.dma_start(right_sb[:], right)
+        nc.gpsimd.dma_start(out=w2_codes[:].bitcast(I32), in_=w2_words[0].bitcast(I32))
+        for q in range(4):
+            nc.gpsimd.dma_start(
+                out=w2_plane[32 * q : 32 * q + 4, :].bitcast(I32),
+                in_=w2_scales[0, 4 * q : 4 * q + 4, :].bitcast(I32),
+            )
+
+        nc.vector.tensor_copy(out=xs_picked[:], in_=xs_table[:].indirect(offs_sb[:]))
+        for r in range(4):
+            nc.scalar.dma_start(
+                out=xs_plane[r:P:32, :].bitcast(I32), in_=xs_picked[8 * r : P : 32, :].bitcast(I32)
+            )
+
+        xw_picked = keep.tile([P, S], U32, name="xw_picked", align_bytes=64)
+        nc.vector.tensor_copy(out=xw_picked[:], in_=xw_table[:].indirect(offs_sb[:]))
+
+        w1_dst = w1_bf[:].rearrange("p (t m j) -> p m t j", t=PACK, j=PACK)
+        w1_src = [raw[:].rearrange("p j (m t) -> p m t j", t=PACK) for raw in w1_raw]
+
+        def round_w1(a, t0, t1, engine):
+            dst, src = w1_dst[:, 64 * a : 64 * (a + 1), t0:t1, :], w1_src[a][:, :, t0:t1, :]
+            if engine == "vector":
+                nc.vector.tensor_copy(out=dst, in_=src)
+            else:
+                nc.scalar.activation(out=dst, in_=src, func=ACT.Copy)
+
+        def quantise_w1(t0, t1):
+            nc.vector.quantize_mx(
+                out=w1_codes[:, P * t0 : P * t1].bitcast(FP8X4),
+                scales=w1_plane[:, P * t0 : P * t1],
+                in_=w1_bf[:, H * t0 : H * t1],
+            )
+
+        h_sb = [keep.tile([P, S], F32, name="h_sb%d" % t, align_bytes=64) for t in range(PACK)]
+
+        def project(t, lo, width, engine):
+            acc = h_psum.tile([P, 512], F32, name="h_acc")
+            nc.tensor.matmul_mx(
+                out=acc[:, 0:width],
+                lhsT=w1_codes[:, P * t : P * (t + 1)].bitcast(FP8X4),
+                lhsT_scale=w1_plane[:, P * t : P * (t + 1)],
+                rhs=xw_picked[:, lo : lo + width].bitcast(FP8X4),
+                rhs_scale=xs_plane[:, lo : lo + width],
+                start=True,
+                stop=True,
+            )
+            if engine == "vector":
+                nc.vector.tensor_copy(out=h_sb[t][:, lo : lo + width], in_=acc[:, 0:width])
+            else:
+                nc.scalar.copy(out=h_sb[t][:, lo : lo + width], in_=acc[:, 0:width])
+
+        round_w1(0, 0, 4, "scalar")
+        round_w1(1, 0, 1, "vector")
+        round_w1(1, 1, 2, "scalar")
+        quantise_w1(0, 1)
+        round_w1(1, 2, 4, "vector")
+        quantise_w1(1, 2)
+        quantise_w1(2, 4)
+        pieces = S // PIECE
+        for g in range(pieces):
+            project(0, g * PIECE, PIECE, "vector" if g == pieces - 1 else "scalar")
+        for t in (1, 2, 3):
+            for lo in (0, 512):
+                project(t, lo, 512, "scalar")
+
+        last_right = keep.tile([P, V + 256], F32, name="last_right", align_bytes=64)
+        h_right = [keep.tile([P, V], F32, name="h_right%d" % t, align_bytes=64)[:] for t in range(PACK - 1)]
+        h_right.append(last_right[:, 0:V])
+        starts = [256, 128, 0]
+        shared = keep.tile([P, 2560], F32, name="shared", align_bytes=64)
+        diff = [
+            keep.tile([P, PACK * n], F32, name="diff%d" % c, align_bytes=64)[:].rearrange("p (t v) -> p t v", t=PACK)
+            for c, n in enumerate(PAIR_CHUNKS[:1])
+        ]
+        diff.append(last_right[:, 256:768].rearrange("p (t v) -> p t v", t=PACK))
+        diff.append(shared[:].rearrange("p (t v) -> p t v", t=PACK)[:, :, 0:128])
+        z_last = keep.tile([P, PACK * 128], BF16, name="z_last", align_bytes=64)
+        z_bf = [shared[:, 0:512].bitcast(BF16), shared[:, 1728:1984].bitcast(BF16), z_last[:]]
+
+        def fetch_right(t):
+            nc.vector.tensor_copy(out=h_right[t], in_=h_sb[t][:].indirect(right_sb[:]))
+
+        def fetch_left(t, c):
+            lo, n = starts[c], PAIR_CHUNKS[c]
+            nc.vector.tensor_tensor(
+                out=diff[c][:, t, :],
+                in0=h_sb[t][:].indirect(left_sb[:, lo // 16 : (lo + n) // 16]),
+                in1=h_right[t][:, lo : lo + n],
+                op=ALU.subtract,
+            )
+
+        def rectify(c, engine):
+            dst = z_bf[c].rearrange("p (v t) -> p v t", t=PACK)
+            src = diff[c].rearrange("p t v -> p v t")
+            if engine == "vector":
+                nc.vector.tensor_scalar(out=dst, in0=src, scalar1=0.0, scalar2=None, op0=ALU.max)
+            else:
+                nc.scalar.activation(out=dst, in_=src, func=ACT.Relu)
+
+        def second_layer(c):
+            lo, n = starts[c], PAIR_CHUNKS[c]
+            z_codes = keep.tile([P, n], U32, name="z_codes%d" % c, align_bytes=64)
+            z_plane = keep.tile([P, n], U8, name="z_plane%d" % c, align_bytes=64)
+            nc.vector.quantize_mx(
+                out=z_codes[:].bitcast(FP8X4),
+                scales=z_plane[:],
+                in_=z_bf[c],
+            )
+            acc = o_psum.tile([P, 2, n], F32, name="o_acc")
+            for half in range(2):
+                nc.tensor.matmul_mx(
+                    out=acc[:, half, :],
+                    lhsT=w2_codes[:, 2 * P * half : 2 * P * (half + 1)].bitcast(FP4X4),
+                    lhsT_scale=w2_plane[:, P * half : P * (half + 1)],
+                    rhs=z_codes[:].bitcast(FP8X4),
+                    rhs_scale=z_plane[:],
+                    start=True,
+                    stop=True,
+                )
+            result = keep.tile([P, 2, n], F32, name="result%d" % c, align_bytes=64)
+            nc.scalar.copy(out=result[:], in_=acc[:])
+            nc.sync.dma_start(
+                out=out[:, lo : lo + n].rearrange("(a p) v -> p a v", p=P), in_=result[:]
+            )
+
+        fetch_right(0)
+        fetch_right(1)
+        fetch_left(0, 0)
+        fetch_left(1, 0)
+        fetch_right(2)
+        fetch_right(3)
+        fetch_left(2, 0)
+        fetch_left(3, 0)
+        rectify(0, "scalar")
+        for t in range(PACK):
+            fetch_left(t, 1)
+        rectify(1, "scalar")
+        second_layer(0)
+        fetch_left(0, 2)
+        fetch_left(1, 2)
+        fetch_left(2, 2)
+        second_layer(1)
+        fetch_left(3, 2)
+        rectify(2, "vector")
+        second_layer(2)

@@ -29,29 +29,25 @@ def tile_picked_phpair_relu_p_kernel(
     with ExitStack() as ctx:
         lists = ctx.enter_context(tc.tile_pool(name="lists", bufs=1))
         keep = ctx.enter_context(tc.tile_pool(name="keep", bufs=1))
-        h_psum = ctx.enter_context(tc.psum_pool(name="h_psum", bufs=6))
-        o_psum = ctx.enter_context(tc.psum_pool(name="o_psum", bufs=2))
+        psum = ctx.enter_context(tc.psum_pool(name="psum", bufs=8))
 
         offs_sb = lists.tile([P, S // 16], U16, name="offs_sb")
         left_sb = lists.tile([P, V // 16], U16, name="left_sb")
         right_sb = lists.tile([P, V // 16], U16, name="right_sb")
 
-        xs_table = keep.tile([P, T], U8, name="xs_table", align_bytes=64)
-        xs_picked = keep.tile([P, S], U8, name="xs_picked", align_bytes=64)
+        xs_table = keep.tile([P, T], U8, name="xs_table", tag="first", align_bytes=64)
+        xs_picked = keep.tile([P, S], U8, name="xs_picked", tag="second", align_bytes=64)
         xs_plane = keep.tile([P, S], U8, name="xs_plane", align_bytes=64)
-        xw_table = keep.tile([P, T], U32, name="xw_table", align_bytes=64)
+        xw_table = keep.tile([P, T], U32, name="xw_table", tag="third", align_bytes=64)
         w1_raw = [keep.tile([P, PACK, H // 2], F32, name="w1_raw%d" % a, align_bytes=64) for a in range(2)]
         w1_bf = keep.tile([P, PACK * H], BF16, name="w1_bf", align_bytes=64)
         w1_codes = keep.tile([P, H], U32, name="w1_codes", align_bytes=64)
         w1_plane = keep.tile([P, H], U8, name="w1_plane", align_bytes=64)
-        w2_codes = keep.tile([P, 2 * N], U8, name="w2_codes", align_bytes=64)
-        w2_plane = keep.tile([P, N], U8, name="w2_plane", align_bytes=64)
 
         warm = keep.tile([P, 16], F32, name="warm", align_bytes=64)
         nc.vector.memset(warm[:, 0:8], 0.0)
         nc.scalar.activation(out=warm[:, 8:16], in_=warm[:, 0:8], func=ACT.Relu)
         nc.vector.memset(xs_plane[:].bitcast(I32), 0)
-        nc.vector.memset(w2_plane[:].bitcast(I32), 0)
 
         nc.sync.dma_start(offs_sb[:], offs)
         nc.sync.dma_start(
@@ -66,12 +62,6 @@ def tile_picked_phpair_relu_p_kernel(
             nc.sync.dma_start(out=w1_raw[a][:], in_=w1_rows[:, :, 256 * a : 256 * (a + 1)])
         nc.sync.dma_start(left_sb[:], left)
         nc.sync.dma_start(right_sb[:], right)
-        nc.gpsimd.dma_start(out=w2_codes[:].bitcast(I32), in_=w2_words[0].bitcast(I32))
-        for q in range(4):
-            nc.gpsimd.dma_start(
-                out=w2_plane[32 * q : 32 * q + 4, :].bitcast(I32),
-                in_=w2_scales[0, 4 * q : 4 * q + 4, :].bitcast(I32),
-            )
 
         nc.vector.tensor_copy(out=xs_picked[:], in_=xs_table[:].indirect(offs_sb[:]))
         for r in range(4):
@@ -79,8 +69,18 @@ def tile_picked_phpair_relu_p_kernel(
                 out=xs_plane[r:P:32, :].bitcast(I32), in_=xs_picked[8 * r : P : 32, :].bitcast(I32)
             )
 
-        xw_picked = keep.tile([P, S], U32, name="xw_picked", align_bytes=64)
+        xw_picked = keep.tile([P, S], U32, name="xw_picked", tag="first", align_bytes=64)
         nc.vector.tensor_copy(out=xw_picked[:], in_=xw_table[:].indirect(offs_sb[:]))
+
+        w2_codes = keep.tile([P, 2 * N], U8, name="w2_codes", tag="third", align_bytes=64)
+        w2_plane = keep.tile([P, N], U8, name="w2_plane", tag="second", align_bytes=64)
+        nc.gpsimd.memset(w2_plane[:].bitcast(I32), 0)
+        nc.sync.dma_start(out=w2_codes[:].bitcast(I32), in_=w2_words[0].bitcast(I32))
+        for q in range(4):
+            nc.sync.dma_start(
+                out=w2_plane[32 * q : 32 * q + 4, :].bitcast(I32),
+                in_=w2_scales[0, 4 * q : 4 * q + 4, :].bitcast(I32),
+            )
 
         w1_dst = w1_bf[:].rearrange("p (t m j) -> p m t j", t=PACK, j=PACK)
         w1_src = [raw[:].rearrange("p j (m t) -> p m t j", t=PACK) for raw in w1_raw]
@@ -102,7 +102,7 @@ def tile_picked_phpair_relu_p_kernel(
         h_sb = [keep.tile([P, S], F32, name="h_sb%d" % t, align_bytes=64) for t in range(PACK)]
 
         def project(t, lo, width, engine):
-            acc = h_psum.tile([P, 512], F32, name="h_acc")
+            acc = psum.tile([P, 512], F32, name="acc")
             nc.tensor.matmul_mx(
                 out=acc[:, 0:width],
                 lhsT=w1_codes[:, P * t : P * (t + 1)].bitcast(FP8X4),
@@ -121,12 +121,13 @@ def tile_picked_phpair_relu_p_kernel(
         round_w1(1, 0, 1, "vector")
         round_w1(1, 1, 2, "scalar")
         quantise_w1(0, 1)
-        round_w1(1, 2, 4, "vector")
+        round_w1(1, 2, 4, "scalar")
         quantise_w1(1, 2)
+        project(0, 0, PIECE, "vector")
         quantise_w1(2, 4)
-        pieces = S // PIECE
-        for g in range(pieces):
-            project(0, g * PIECE, PIECE, "vector" if g == pieces - 1 else "scalar")
+        project(0, PIECE, PIECE, "scalar")
+        project(0, 2 * PIECE, PIECE, "scalar")
+        project(0, 3 * PIECE, PIECE, "vector")
         for t in (1, 2, 3):
             for lo in (0, 512):
                 project(t, lo, 512, "scalar")
@@ -146,7 +147,11 @@ def tile_picked_phpair_relu_p_kernel(
         z_bf = [shared[:, 0:512].bitcast(BF16), shared[:, 1728:1984].bitcast(BF16), z_last[:]]
 
         def fetch_right(t):
-            nc.vector.tensor_copy(out=h_right[t], in_=h_sb[t][:].indirect(right_sb[:]))
+            for lo in (256, 0):
+                nc.vector.tensor_copy(
+                    out=h_right[t][:, lo : lo + 256],
+                    in_=h_sb[t][:].indirect(right_sb[:, lo // 16 : (lo + 256) // 16]),
+                )
 
         def fetch_left(t, c):
             lo, n = starts[c], PAIR_CHUNKS[c]
@@ -174,10 +179,10 @@ def tile_picked_phpair_relu_p_kernel(
                 scales=z_plane[:],
                 in_=z_bf[c],
             )
-            acc = o_psum.tile([P, 2, n], F32, name="o_acc")
-            for half in range(2):
+
+            def multiply(half, acc):
                 nc.tensor.matmul_mx(
-                    out=acc[:, half, :],
+                    out=acc,
                     lhsT=w2_codes[:, 2 * P * half : 2 * P * (half + 1)].bitcast(FP4X4),
                     lhsT_scale=w2_plane[:, P * half : P * (half + 1)],
                     rhs=z_codes[:].bitcast(FP8X4),
@@ -185,20 +190,31 @@ def tile_picked_phpair_relu_p_kernel(
                     start=True,
                     stop=True,
                 )
-            result = keep.tile([P, 2, n], F32, name="result%d" % c, align_bytes=64)
-            nc.scalar.copy(out=result[:], in_=acc[:])
-            nc.sync.dma_start(
-                out=out[:, lo : lo + n].rearrange("(a p) v -> p a v", p=P), in_=result[:]
-            )
 
-        fetch_right(0)
-        fetch_right(1)
-        fetch_left(0, 0)
-        fetch_left(1, 0)
-        fetch_right(2)
-        fetch_right(3)
-        fetch_left(2, 0)
-        fetch_left(3, 0)
+            if c < len(PAIR_CHUNKS) - 1:
+                acc = psum.tile([P, 2, n], F32, name="acc")
+                for half in range(2):
+                    multiply(half, acc[:, half, :])
+                result = keep.tile([P, 2, n], F32, name="result%d" % c, align_bytes=64)
+                nc.scalar.copy(out=result[:], in_=acc[:])
+                nc.sync.dma_start(
+                    out=out[:, lo : lo + n].rearrange("(a p) v -> p a v", p=P), in_=result[:]
+                )
+            else:
+                for half in range(2):
+                    acc = psum.tile([P, n], F32, name="acc")
+                    multiply(half, acc[:])
+                    result = keep.tile([P, n], F32, name="last%d" % half, align_bytes=64)
+                    if half == 0:
+                        nc.scalar.copy(out=result[:], in_=acc[:])
+                        nc.scalar.dma_start(out=out[0:P, lo : lo + n], in_=result[:])
+                    else:
+                        nc.vector.tensor_copy(out=result[:], in_=acc[:])
+                        nc.sync.dma_start(out=out[P : 2 * P, lo : lo + n], in_=result[:])
+
+        for t in range(PACK):
+            fetch_right(t)
+            fetch_left(t, 0)
         rectify(0, "scalar")
         for t in range(PACK):
             fetch_left(t, 1)

@@ -39,7 +39,7 @@ def tile_picked_phpair_relu_p_kernel(
         xs_picked = keep.tile([P, S], U8, name="xs_picked", tag="second", align_bytes=64)
         xs_plane = keep.tile([P, S], U8, name="xs_plane", align_bytes=64)
         xw_table = keep.tile([P, T], U32, name="xw_table", tag="third", align_bytes=64)
-        w1_raw = [keep.tile([P, PACK, H // 2], F32, name="w1_raw%d" % a, align_bytes=64) for a in range(2)]
+        w1_raw = [keep.tile([P, 2, H], F32, name="w1_raw%d" % a, align_bytes=64) for a in range(2)]
         w1_bf = keep.tile([P, PACK * H], BF16, name="w1_bf", align_bytes=64)
         w1_codes = keep.tile([P, H], U32, name="w1_codes", align_bytes=64)
         w1_plane = keep.tile([P, H], U8, name="w1_plane", align_bytes=64)
@@ -59,7 +59,7 @@ def tile_picked_phpair_relu_p_kernel(
         )
         w1_rows = w1.rearrange("(p j) c -> p j c", j=PACK)
         for a in range(2):
-            nc.sync.dma_start(out=w1_raw[a][:], in_=w1_rows[:, :, 256 * a : 256 * (a + 1)])
+            nc.sync.dma_start(out=w1_raw[a][:], in_=w1_rows[:, 2 * a : 2 * a + 2, :])
         nc.sync.dma_start(left_sb[:], left)
         nc.sync.dma_start(right_sb[:], right)
 
@@ -86,7 +86,7 @@ def tile_picked_phpair_relu_p_kernel(
         w1_src = [raw[:].rearrange("p j (m t) -> p m t j", t=PACK) for raw in w1_raw]
 
         def round_w1(a, t0, t1, engine):
-            dst, src = w1_dst[:, 64 * a : 64 * (a + 1), t0:t1, :], w1_src[a][:, :, t0:t1, :]
+            dst, src = w1_dst[:, :, t0:t1, 2 * a : 2 * a + 2], w1_src[a][:, :, t0:t1, :]
             if engine == "vector":
                 nc.vector.tensor_copy(out=dst, in_=src)
             else:
@@ -117,40 +117,42 @@ def tile_picked_phpair_relu_p_kernel(
             else:
                 nc.scalar.copy(out=h_sb[t][:, lo : lo + width], in_=acc[:, 0:width])
 
-        round_w1(0, 0, 4, "scalar")
+        round_w1(0, 0, 1, "scalar")
+        round_w1(0, 1, 4, "scalar")
         round_w1(1, 0, 1, "vector")
         round_w1(1, 1, 2, "scalar")
         quantise_w1(0, 1)
         round_w1(1, 2, 4, "scalar")
-        quantise_w1(1, 2)
         project(0, 0, PIECE, "vector")
-        quantise_w1(2, 4)
-        project(0, PIECE, PIECE, "scalar")
+        quantise_w1(1, 2)
+        project(0, PIECE, PIECE, "vector")
         project(0, 2 * PIECE, PIECE, "scalar")
         project(0, 3 * PIECE, PIECE, "vector")
+        quantise_w1(2, 4)
         for t in (1, 2, 3):
             for lo in (0, 512):
                 project(t, lo, 512, "scalar")
 
-        last_right = keep.tile([P, V + 256], F32, name="last_right", align_bytes=64)
-        h_right = [keep.tile([P, V], F32, name="h_right%d" % t, align_bytes=64)[:] for t in range(PACK - 1)]
-        h_right.append(last_right[:, 0:V])
-        starts = [256, 128, 0]
-        shared = keep.tile([P, 2560], F32, name="shared", align_bytes=64)
+        starts = [256, 0, 128]
+        shared = keep.tile([P, 1024], F32, name="shared", align_bytes=64)
+        second = keep.tile([P, 512], F32, name="diff_second", align_bytes=64)
+        right_first = [keep.tile([P, 256], F32, name="right_first%d" % t, align_bytes=64)[:] for t in range(3)]
+        right_first.append(second[:, 120:376])
+        right_rest = [keep.tile([P, 256], F32, name="right_rest%d" % t, align_bytes=64)[:] for t in range(3)]
+        right_rest.append(shared[:, 0:256])
+        first = keep.tile([P, 1024], F32, name="diff_first", align_bytes=64)
         diff = [
-            keep.tile([P, PACK * n], F32, name="diff%d" % c, align_bytes=64)[:].rearrange("p (t v) -> p t v", t=PACK)
-            for c, n in enumerate(PAIR_CHUNKS[:1])
+            first[:].rearrange("p (t v) -> p t v", t=PACK),
+            second[:].rearrange("p (t v) -> p t v", t=PACK),
+            shared[:].rearrange("p (t v) -> p t v", t=PACK)[:, :, 0:128],
         ]
-        diff.append(last_right[:, 256:768].rearrange("p (t v) -> p t v", t=PACK))
-        diff.append(shared[:].rearrange("p (t v) -> p t v", t=PACK)[:, :, 0:128])
-        z_last = keep.tile([P, PACK * 128], BF16, name="z_last", align_bytes=64)
-        z_bf = [shared[:, 0:512].bitcast(BF16), shared[:, 1728:1984].bitcast(BF16), z_last[:]]
+        z_small = keep.tile([P, PACK * 128], BF16, name="z_small", align_bytes=64)
+        z_bf = [shared[:, 320:832].bitcast(BF16), z_small[:], z_small[:]]
 
         def fetch_right(t):
-            for lo in (256, 0):
+            for lo, picked in ((256, right_first[t]), (0, right_rest[t])):
                 nc.vector.tensor_copy(
-                    out=h_right[t][:, lo : lo + 256],
-                    in_=h_sb[t][:].indirect(right_sb[:, lo // 16 : (lo + 256) // 16]),
+                    out=picked, in_=h_sb[t][:].indirect(right_sb[:, lo // 16 : (lo + 256) // 16])
                 )
 
         def fetch_left(t, c):
@@ -158,7 +160,7 @@ def tile_picked_phpair_relu_p_kernel(
             nc.vector.tensor_tensor(
                 out=diff[c][:, t, :],
                 in0=h_sb[t][:].indirect(left_sb[:, lo // 16 : (lo + n) // 16]),
-                in1=h_right[t][:, lo : lo + n],
+                in1=right_first[t] if c == 0 else right_rest[t][:, lo : lo + n],
                 op=ALU.subtract,
             )
 
@@ -219,11 +221,11 @@ def tile_picked_phpair_relu_p_kernel(
         for t in range(PACK):
             fetch_left(t, 1)
         rectify(1, "scalar")
-        second_layer(0)
         fetch_left(0, 2)
+        second_layer(0)
         fetch_left(1, 2)
         fetch_left(2, 2)
-        second_layer(1)
         fetch_left(3, 2)
+        second_layer(1)
         rectify(2, "vector")
         second_layer(2)

@@ -117,18 +117,18 @@ def tile_picked_phpair_relu_p_kernel(
             else:
                 nc.scalar.copy(out=h_sb[t][:, lo : lo + width], in_=acc[:, 0:width])
 
-        round_w1(0, 0, 1, "scalar")
-        round_w1(0, 1, 4, "scalar")
+        round_w1(0, 0, 2, "scalar")
+        round_w1(0, 2, 4, "scalar")
         round_w1(1, 0, 1, "vector")
-        round_w1(1, 1, 2, "scalar")
+        round_w1(1, 1, 2, "vector")
         quantise_w1(0, 1)
+        quantise_w1(1, 2)
         round_w1(1, 2, 4, "scalar")
         project(0, 0, PIECE, "vector")
-        quantise_w1(1, 2)
-        project(0, PIECE, PIECE, "vector")
+        quantise_w1(2, 4)
+        project(0, PIECE, PIECE, "scalar")
         project(0, 2 * PIECE, PIECE, "scalar")
         project(0, 3 * PIECE, PIECE, "vector")
-        quantise_w1(2, 4)
         for t in (1, 2, 3):
             for lo in (0, 512):
                 project(t, lo, 512, "scalar")
@@ -165,8 +165,8 @@ def tile_picked_phpair_relu_p_kernel(
             )
 
         def rectify(c, engine):
-            dst = z_bf[c].rearrange("p (v t) -> p v t", t=PACK)
-            src = diff[c].rearrange("p t v -> p v t")
+            dst = z_bf[c].rearrange("p (a i t) -> p a t i", i=4, t=PACK)
+            src = diff[c].rearrange("p t (a i) -> p a t i", i=4)
             if engine == "vector":
                 nc.vector.tensor_scalar(out=dst, in0=src, scalar1=0.0, scalar2=None, op0=ALU.max)
             else:

@@ -40,7 +40,7 @@ def tile_picked_phpair_relu_p_kernel(
         xs_plane = keep.tile([P, S], U8, name="xs_plane", align_bytes=64)
         xw_table = keep.tile([P, T], U32, name="xw_table", tag="third", align_bytes=64)
         w1_raw = [keep.tile([P, 2, H], F32, name="w1_raw%d" % a, align_bytes=64) for a in range(2)]
-        w1_bf = keep.tile([P, PACK * H], BF16, name="w1_bf", align_bytes=64)
+        w1_bf = keep.tile([P, 3 * H], BF16, name="w1_bf", align_bytes=64)
         w1_codes = keep.tile([P, H], U32, name="w1_codes", align_bytes=64)
         w1_plane = keep.tile([P, H], U8, name="w1_plane", align_bytes=64)
 
@@ -82,21 +82,23 @@ def tile_picked_phpair_relu_p_kernel(
                 in_=w2_scales[0, 4 * q : 4 * q + 4, :].bitcast(I32),
             )
 
-        w1_dst = w1_bf[:].rearrange("p (t m j) -> p m t j", t=PACK, j=PACK)
         w1_src = [raw[:].rearrange("p j (m t) -> p m t j", t=PACK) for raw in w1_raw]
+        w1_dst = w1_bf[:].rearrange("p (s m j) -> p m s j", s=3, j=PACK)
 
         def round_w1(a, t0, t1, engine):
-            dst, src = w1_dst[:, :, t0:t1, 2 * a : 2 * a + 2], w1_src[a][:, :, t0:t1, :]
+            s0 = t0 % 3
+            dst, src = w1_dst[:, :, s0 : s0 + t1 - t0, 2 * a : 2 * a + 2], w1_src[a][:, :, t0:t1, :]
             if engine == "vector":
                 nc.vector.tensor_copy(out=dst, in_=src)
             else:
                 nc.scalar.activation(out=dst, in_=src, func=ACT.Copy)
 
         def quantise_w1(t0, t1):
+            s0 = t0 % 3
             nc.vector.quantize_mx(
                 out=w1_codes[:, P * t0 : P * t1].bitcast(FP8X4),
                 scales=w1_plane[:, P * t0 : P * t1],
-                in_=w1_bf[:, H * t0 : H * t1],
+                in_=w1_bf[:, H * s0 : H * (s0 + t1 - t0)],
             )
 
         h_sb = [keep.tile([P, S], F32, name="h_sb%d" % t, align_bytes=64) for t in range(PACK)]
@@ -117,37 +119,43 @@ def tile_picked_phpair_relu_p_kernel(
             else:
                 nc.scalar.copy(out=h_sb[t][:, lo : lo + width], in_=acc[:, 0:width])
 
-        round_w1(0, 0, 2, "scalar")
-        round_w1(0, 2, 4, "scalar")
-        round_w1(1, 0, 1, "vector")
-        round_w1(1, 1, 2, "vector")
+        round_w1(0, 0, 3, "scalar")
+        round_w1(1, 0, 1, "scalar")
         quantise_w1(0, 1)
-        quantise_w1(1, 2)
-        round_w1(1, 2, 4, "scalar")
-        project(0, 0, PIECE, "vector")
-        quantise_w1(2, 4)
-        project(0, PIECE, PIECE, "scalar")
-        project(0, 2 * PIECE, PIECE, "scalar")
-        project(0, 3 * PIECE, PIECE, "vector")
+        round_w1(1, 1, 3, "scalar")
+        round_w1(0, 3, 4, "vector")
+        round_w1(1, 3, 4, "vector")
+        quantise_w1(1, 3)
+        quantise_w1(3, 4)
+        project(0, 0, 256, "scalar")
+        project(0, 256, 256, "vector")
+        project(0, 512, 256, "scalar")
+        project(0, 768, 128, "vector")
+        project(0, 896, 128, "scalar")
         for t in (1, 2, 3):
             for lo in (0, 512):
                 project(t, lo, 512, "scalar")
 
         starts = [256, 0, 128]
-        shared = keep.tile([P, 1024], F32, name="shared", align_bytes=64)
-        second = keep.tile([P, 512], F32, name="diff_second", align_bytes=64)
-        right_first = [keep.tile([P, 256], F32, name="right_first%d" % t, align_bytes=64)[:] for t in range(3)]
-        right_first.append(second[:, 120:376])
-        right_rest = [keep.tile([P, 256], F32, name="right_rest%d" % t, align_bytes=64)[:] for t in range(3)]
-        right_rest.append(shared[:, 0:256])
         first = keep.tile([P, 1024], F32, name="diff_first", align_bytes=64)
+        second = keep.tile([P, 512], F32, name="diff_second", align_bytes=64)
+        third = keep.tile([P, 512], F32, name="diff_third", align_bytes=64)
+        right_first = [keep.tile([P, 256], F32, name="right_first%d" % t, align_bytes=64)[:] for t in range(3)]
+        right_first.append(second[:, 64:320])
+        right_rest = [keep.tile([P, 256], F32, name="right_rest%d" % t, align_bytes=64)[:] for t in range(3)]
+        right_rest.append(third[:, 0:256])
+        first_diff = first[:].rearrange("p (t v) -> p t v", t=PACK)
+        second_diff = second[:].rearrange("p (t v) -> p t v", t=PACK)
+        third_low = first[:, 0:256].rearrange("p (t v) -> p t v", t=2)
+        third_high = third[:].rearrange("p (t v) -> p t v", t=2)[:, :, 0:128]
         diff = [
-            first[:].rearrange("p (t v) -> p t v", t=PACK),
-            second[:].rearrange("p (t v) -> p t v", t=PACK),
-            shared[:].rearrange("p (t v) -> p t v", t=PACK)[:, :, 0:128],
+            [first_diff[:, t, :] for t in range(PACK)],
+            [second_diff[:, t, :] for t in range(PACK)],
+            [third_low[:, 0, :], third_low[:, 1, :], third_high[:, 0, :], third_high[:, 1, :]],
         ]
-        z_small = keep.tile([P, PACK * 128], BF16, name="z_small", align_bytes=64)
-        z_bf = [shared[:, 320:832].bitcast(BF16), z_small[:], z_small[:]]
+        z_bf = [
+            keep.tile([P, PACK * n], BF16, name="z_bf%d" % c, align_bytes=64)[:] for c, n in enumerate(PAIR_CHUNKS)
+        ]
 
         def fetch_right(t):
             for lo, picked in ((256, right_first[t]), (0, right_rest[t])):
@@ -158,15 +166,15 @@ def tile_picked_phpair_relu_p_kernel(
         def fetch_left(t, c):
             lo, n = starts[c], PAIR_CHUNKS[c]
             nc.vector.tensor_tensor(
-                out=diff[c][:, t, :],
+                out=diff[c][t],
                 in0=h_sb[t][:].indirect(left_sb[:, lo // 16 : (lo + n) // 16]),
                 in1=right_first[t] if c == 0 else right_rest[t][:, lo : lo + n],
                 op=ALU.subtract,
             )
 
-        def rectify(c, engine):
-            dst = z_bf[c].rearrange("p (a i t) -> p a t i", i=4, t=PACK)
-            src = diff[c].rearrange("p t (a i) -> p a t i", i=4)
+        def rectify(c, planes, t0, t1, engine):
+            dst = z_bf[c].rearrange("p (a i t) -> p a t i", i=4, t=PACK)[:, :, t0:t1, :]
+            src = planes.rearrange("p t (a i) -> p a t i", i=4)
             if engine == "vector":
                 nc.vector.tensor_scalar(out=dst, in0=src, scalar1=0.0, scalar2=None, op0=ALU.max)
             else:
@@ -217,15 +225,16 @@ def tile_picked_phpair_relu_p_kernel(
         for t in range(PACK):
             fetch_right(t)
             fetch_left(t, 0)
-        rectify(0, "scalar")
-        for t in range(PACK):
+        rectify(0, first_diff, 0, 4, "scalar")
+        for t in (3, 0, 1, 2):
             fetch_left(t, 1)
-        rectify(1, "scalar")
-        fetch_left(0, 2)
-        second_layer(0)
-        fetch_left(1, 2)
-        fetch_left(2, 2)
+        rectify(1, second_diff, 0, 4, "scalar")
         fetch_left(3, 2)
+        fetch_left(2, 2)
+        rectify(2, third_high, 2, 4, "scalar")
+        second_layer(0)
+        fetch_left(0, 2)
+        fetch_left(1, 2)
         second_layer(1)
-        rectify(2, "vector")
+        rectify(2, third_low, 0, 2, "vector")
         second_layer(2)

@@ -40,28 +40,26 @@ def tile_picked_phpair_relu_p_kernel(
         xs_plane = keep.tile([P, S], U8, name="xs_plane", align_bytes=64)
         xw_table = keep.tile([P, T], U32, name="xw_table", tag="third", align_bytes=64)
         w1_raw = [keep.tile([P, 2, H], F32, name="w1_raw%d" % a, align_bytes=64) for a in range(2)]
-        w1_bf = keep.tile([P, 3 * H], BF16, name="w1_bf", align_bytes=64)
+        w1_bf = keep.tile([P, 7 * H // 2], BF16, name="w1_bf", align_bytes=64)
         w1_codes = keep.tile([P, H], U32, name="w1_codes", align_bytes=64)
         w1_plane = keep.tile([P, H], U8, name="w1_plane", align_bytes=64)
 
         warm = keep.tile([P, 16], F32, name="warm", align_bytes=64)
+        nc.vector.memset(xs_table[:].bitcast(I32), 0)
         nc.vector.memset(warm[:, 0:8], 0.0)
         nc.scalar.activation(out=warm[:, 8:16], in_=warm[:, 0:8], func=ACT.Relu)
         nc.vector.memset(xs_plane[:].bitcast(I32), 0)
 
         nc.sync.dma_start(offs_sb[:], offs)
-        nc.sync.dma_start(
-            out=xs_table[:].bitcast(I32),
-            in_=x_scales[0].bitcast(I32).unsqueeze(1).broadcast_to([16, 8, T // 4]),
-        )
+        nc.sync.dma_start(left_sb[:], left)
+        nc.sync.dma_start(right_sb[:], right)
+        nc.sync.dma_start(out=xs_table[0:P:8, :].bitcast(I32), in_=x_scales[0].bitcast(I32))
         nc.sync.dma_start(
             out=xw_table[:].bitcast(I32), in_=x_words[0].rearrange("p c r -> p (c r)").bitcast(I32)
         )
         w1_rows = w1.rearrange("(p j) c -> p j c", j=PACK)
         for a in range(2):
             nc.sync.dma_start(out=w1_raw[a][:], in_=w1_rows[:, 2 * a : 2 * a + 2, :])
-        nc.sync.dma_start(left_sb[:], left)
-        nc.sync.dma_start(right_sb[:], right)
 
         nc.vector.tensor_copy(out=xs_picked[:], in_=xs_table[:].indirect(offs_sb[:]))
         for r in range(4):
@@ -83,22 +81,23 @@ def tile_picked_phpair_relu_p_kernel(
             )
 
         w1_src = [raw[:].rearrange("p j (m t) -> p m t j", t=PACK) for raw in w1_raw]
-        w1_dst = w1_bf[:].rearrange("p (s m j) -> p m s j", s=3, j=PACK)
+        stage_at = (3 * H // 2, 5 * H // 2, 0, H)
 
         def round_w1(a, t0, t1, engine):
-            s0 = t0 % 3
-            dst, src = w1_dst[:, :, s0 : s0 + t1 - t0, 2 * a : 2 * a + 2], w1_src[a][:, :, t0:t1, :]
+            at = stage_at[t0]
+            staged = w1_bf[:, at : at + H * (t1 - t0)].rearrange("p (s m j) -> p m s j", s=t1 - t0, j=PACK)
+            dst, src = staged[:, :, :, 2 * a : 2 * a + 2], w1_src[a][:, :, t0:t1, :]
             if engine == "vector":
                 nc.vector.tensor_copy(out=dst, in_=src)
             else:
                 nc.scalar.activation(out=dst, in_=src, func=ACT.Copy)
 
         def quantise_w1(t0, t1):
-            s0 = t0 % 3
+            at = stage_at[t0]
             nc.vector.quantize_mx(
                 out=w1_codes[:, P * t0 : P * t1].bitcast(FP8X4),
                 scales=w1_plane[:, P * t0 : P * t1],
-                in_=w1_bf[:, H * s0 : H * (s0 + t1 - t0)],
+                in_=w1_bf[:, at : at + H * (t1 - t0)],
             )
 
         h_sb = [keep.tile([P, S], F32, name="h_sb%d" % t, align_bytes=64) for t in range(PACK)]
@@ -119,16 +118,16 @@ def tile_picked_phpair_relu_p_kernel(
             else:
                 nc.scalar.copy(out=h_sb[t][:, lo : lo + width], in_=acc[:, 0:width])
 
-        round_w1(0, 0, 3, "scalar")
+        round_w1(0, 0, 2, "scalar")
         round_w1(1, 0, 1, "scalar")
         quantise_w1(0, 1)
-        round_w1(1, 1, 3, "scalar")
-        round_w1(0, 3, 4, "vector")
-        round_w1(1, 3, 4, "vector")
-        quantise_w1(1, 3)
-        quantise_w1(3, 4)
+        round_w1(1, 1, 2, "scalar")
+        round_w1(0, 2, 4, "vector")
+        round_w1(1, 2, 4, "vector")
+        quantise_w1(1, 2)
+        quantise_w1(2, 4)
         project(0, 0, 256, "scalar")
-        project(0, 256, 256, "vector")
+        project(0, 256, 256, "scalar")
         project(0, 512, 256, "scalar")
         project(0, 768, 128, "vector")
         project(0, 896, 128, "scalar")

@@ -29,16 +29,17 @@ def tile_picked_phpair_relu_p_kernel(
     with ExitStack() as ctx:
         lists = ctx.enter_context(tc.tile_pool(name="lists", bufs=1))
         keep = ctx.enter_context(tc.tile_pool(name="keep", bufs=1))
-        psum = ctx.enter_context(tc.psum_pool(name="psum", bufs=8))
+        psum = ctx.enter_context(tc.psum_pool(name="psum", bufs=7))
+        psum_out = ctx.enter_context(tc.psum_pool(name="psum_out", bufs=1))
 
         offs_sb = lists.tile([P, S // 16], U16, name="offs_sb")
         left_sb = lists.tile([P, V // 16], U16, name="left_sb")
         right_sb = lists.tile([P, V // 16], U16, name="right_sb")
 
-        xs_table = keep.tile([P, T], U8, name="xs_table", tag="first", align_bytes=64)
-        xs_picked = keep.tile([P, S], U8, name="xs_picked", tag="second", align_bytes=64)
-        xs_plane = keep.tile([P, S], U8, name="xs_plane", align_bytes=64)
-        xw_table = keep.tile([P, T], U32, name="xw_table", tag="third", align_bytes=64)
+        xs_table = keep.tile([P, T], U8, name="xs_table", align_bytes=64)
+        xs_picked = keep.tile([P, S], U8, name="xs_picked", align_bytes=64)
+        xs_plane = keep.tile([P, S], U8, name="xs_plane", tag="plane", align_bytes=64)
+        xw_table = keep.tile([P, T], U32, name="xw_table", align_bytes=64)
         w1_raw = [keep.tile([P, 2, H], F32, name="w1_raw%d" % a, align_bytes=64) for a in range(2)]
         w1_bf = keep.tile([P, 7 * H // 2], BF16, name="w1_bf", align_bytes=64)
         w1_codes = keep.tile([P, H], U32, name="w1_codes", align_bytes=64)
@@ -67,26 +68,16 @@ def tile_picked_phpair_relu_p_kernel(
                 out=xs_plane[r:P:32, :].bitcast(I32), in_=xs_picked[8 * r : P : 32, :].bitcast(I32)
             )
 
-        xw_picked = keep.tile([P, S], U32, name="xw_picked", tag="first", align_bytes=64)
+        xw_picked = keep.tile([P, S], U32, name="xw_picked", tag="words", align_bytes=64)
         nc.vector.tensor_copy(out=xw_picked[:], in_=xw_table[:].indirect(offs_sb[:]))
-
-        w2_codes = keep.tile([P, 2 * N], U8, name="w2_codes", tag="third", align_bytes=64)
-        w2_plane = keep.tile([P, N], U8, name="w2_plane", tag="second", align_bytes=64)
-        nc.gpsimd.memset(w2_plane[:].bitcast(I32), 0)
-        nc.sync.dma_start(out=w2_codes[:].bitcast(I32), in_=w2_words[0].bitcast(I32))
-        for q in range(4):
-            nc.sync.dma_start(
-                out=w2_plane[32 * q : 32 * q + 4, :].bitcast(I32),
-                in_=w2_scales[0, 4 * q : 4 * q + 4, :].bitcast(I32),
-            )
 
         w1_src = [raw[:].rearrange("p j (m t) -> p m t j", t=PACK) for raw in w1_raw]
         stage_at = (3 * H // 2, 5 * H // 2, 0, H)
 
-        def round_w1(a, t0, t1, engine):
+        def round_w1(a, t0, t1, engine, m0=0, m1=P):
             at = stage_at[t0]
             staged = w1_bf[:, at : at + H * (t1 - t0)].rearrange("p (s m j) -> p m s j", s=t1 - t0, j=PACK)
-            dst, src = staged[:, :, :, 2 * a : 2 * a + 2], w1_src[a][:, :, t0:t1, :]
+            dst, src = staged[:, m0:m1, :, 2 * a : 2 * a + 2], w1_src[a][:, m0:m1, t0:t1, :]
             if engine == "vector":
                 nc.vector.tensor_copy(out=dst, in_=src)
             else:
@@ -119,7 +110,8 @@ def tile_picked_phpair_relu_p_kernel(
                 nc.scalar.copy(out=h_sb[t][:, lo : lo + width], in_=acc[:, 0:width])
 
         round_w1(0, 0, 2, "scalar")
-        round_w1(1, 0, 1, "scalar")
+        round_w1(1, 0, 1, "scalar", 0, P // 2)
+        round_w1(1, 0, 1, "vector", P // 2, P)
         quantise_w1(0, 1)
         round_w1(1, 1, 2, "scalar")
         round_w1(0, 2, 4, "vector")
@@ -135,18 +127,26 @@ def tile_picked_phpair_relu_p_kernel(
             for lo in (0, 512):
                 project(t, lo, 512, "scalar")
 
+        w2_codes = keep.tile([P, 2 * N], U8, name="w2_codes", tag="words", align_bytes=64)
+        w2_plane = keep.tile([P, N], U8, name="w2_plane", tag="plane", align_bytes=64)
+        nc.gpsimd.memset(w2_plane[:].bitcast(I32), 0)
+        nc.sync.dma_start(out=w2_codes[:].bitcast(I32), in_=w2_words[0].bitcast(I32))
+        for q in range(4):
+            nc.sync.dma_start(
+                out=w2_plane[32 * q : 32 * q + 4, :].bitcast(I32),
+                in_=w2_scales[0, 4 * q : 4 * q + 4, :].bitcast(I32),
+            )
+
         starts = [256, 0, 128]
-        first = keep.tile([P, 1024], F32, name="diff_first", align_bytes=64)
+        first = keep.tile([P, 1152], F32, name="diff_first", align_bytes=64)
         second = keep.tile([P, 512], F32, name="diff_second", align_bytes=64)
-        third = keep.tile([P, 512], F32, name="diff_third", align_bytes=64)
         right_first = [keep.tile([P, 256], F32, name="right_first%d" % t, align_bytes=64)[:] for t in range(3)]
         right_first.append(second[:, 64:320])
-        right_rest = [keep.tile([P, 256], F32, name="right_rest%d" % t, align_bytes=64)[:] for t in range(3)]
-        right_rest.append(third[:, 0:256])
-        first_diff = first[:].rearrange("p (t v) -> p t v", t=PACK)
+        right_rest = [keep.tile([P, 256], F32, name="right_rest%d" % t, align_bytes=64)[:] for t in range(PACK)]
+        first_diff = first[:, 0:1024].rearrange("p (t v) -> p t v", t=PACK)
         second_diff = second[:].rearrange("p (t v) -> p t v", t=PACK)
-        third_low = first[:, 0:256].rearrange("p (t v) -> p t v", t=2)
-        third_high = third[:].rearrange("p (t v) -> p t v", t=2)[:, :, 0:128]
+        third_low = first[:, 512:768].rearrange("p (t v) -> p t v", t=2)
+        third_high = first[:, 896:1152].rearrange("p (t v) -> p t v", t=2)
         diff = [
             [first_diff[:, t, :] for t in range(PACK)],
             [second_diff[:, t, :] for t in range(PACK)],
@@ -201,17 +201,17 @@ def tile_picked_phpair_relu_p_kernel(
                 )
 
             if c < len(PAIR_CHUNKS) - 1:
-                acc = psum.tile([P, 2, n], F32, name="acc")
+                acc = (psum if c else psum_out).tile([P, 2, n], F32, name="acc")
                 for half in range(2):
                     multiply(half, acc[:, half, :])
                 result = keep.tile([P, 2, n], F32, name="result%d" % c, align_bytes=64)
                 nc.scalar.copy(out=result[:], in_=acc[:])
-                nc.sync.dma_start(
+                (nc.scalar if c else nc.sync).dma_start(
                     out=out[:, lo : lo + n].rearrange("(a p) v -> p a v", p=P), in_=result[:]
                 )
             else:
                 for half in range(2):
-                    acc = psum.tile([P, n], F32, name="acc")
+                    acc = (psum_out if half else psum).tile([P, n], F32, name="acc")
                     multiply(half, acc[:])
                     result = keep.tile([P, n], F32, name="last%d" % half, align_bytes=64)
                     if half == 0:
@@ -224,14 +224,15 @@ def tile_picked_phpair_relu_p_kernel(
         for t in range(PACK):
             fetch_right(t)
             fetch_left(t, 0)
-        rectify(0, first_diff, 0, 4, "scalar")
+            if t % 2:
+                rectify(0, first_diff[:, t - 1 : t + 1, :], t - 1, t + 1, "scalar")
         for t in (3, 0, 1, 2):
             fetch_left(t, 1)
         rectify(1, second_diff, 0, 4, "scalar")
         fetch_left(3, 2)
+        second_layer(0)
         fetch_left(2, 2)
         rectify(2, third_high, 2, 4, "scalar")
-        second_layer(0)
         fetch_left(0, 2)
         fetch_left(1, 2)
         second_layer(1)

@@ -18,7 +18,7 @@ ACT = mybir.ActivationFunctionType
 
 P = 128
 PACK = 4
-PIECE = 256
+X_EARLY = 384
 PAIR_CHUNKS = (256, 128, 128)
 
 
@@ -40,8 +40,8 @@ def tile_picked_phpair_relu_p_kernel(
         xs_picked = keep.tile([P, S], U8, name="xs_picked", align_bytes=64)
         xs_plane = keep.tile([P, S], U8, name="xs_plane", tag="plane", align_bytes=64)
         xw_table = keep.tile([P, T], U32, name="xw_table", align_bytes=64)
-        w1_raw = [keep.tile([P, 2, H], F32, name="w1_raw%d" % a, align_bytes=64) for a in range(2)]
-        w1_bf = keep.tile([P, 7 * H // 2], BF16, name="w1_bf", align_bytes=64)
+        w1_raw = keep.tile([P, PACK * H], F32, name="w1_raw", align_bytes=64)
+        w1_bf = keep.tile([P, PACK * H], BF16, name="w1_bf", align_bytes=64)
         w1_codes = keep.tile([P, H], U32, name="w1_codes", align_bytes=64)
         w1_plane = keep.tile([P, H], U8, name="w1_plane", align_bytes=64)
 
@@ -51,16 +51,16 @@ def tile_picked_phpair_relu_p_kernel(
         nc.scalar.activation(out=warm[:, 8:16], in_=warm[:, 0:8], func=ACT.Relu)
         nc.vector.memset(xs_plane[:].bitcast(I32), 0)
 
+        x_rows = x_words[0].rearrange("p c r -> p (c r)").bitcast(I32)
         nc.sync.dma_start(offs_sb[:], offs)
+        nc.sync.dma_start(out=xw_table[:, 0:X_EARLY].bitcast(I32), in_=x_rows[:, 0:X_EARLY])
         nc.sync.dma_start(left_sb[:], left)
         nc.sync.dma_start(right_sb[:], right)
         nc.sync.dma_start(out=xs_table[0:P:8, :].bitcast(I32), in_=x_scales[0].bitcast(I32))
-        nc.sync.dma_start(
-            out=xw_table[:].bitcast(I32), in_=x_words[0].rearrange("p c r -> p (c r)").bitcast(I32)
-        )
-        w1_rows = w1.rearrange("(p j) c -> p j c", j=PACK)
-        for a in range(2):
-            nc.sync.dma_start(out=w1_raw[a][:], in_=w1_rows[:, 2 * a : 2 * a + 2, :])
+        nc.sync.dma_start(out=xw_table[:, X_EARLY:T].bitcast(I32), in_=x_rows[:, X_EARLY:T])
+        w1_rows = w1.rearrange("(p j) c -> p (j c)", j=PACK)
+        for lo in (0, 2 * H):
+            nc.sync.dma_start(out=w1_raw[:, lo : lo + 2 * H], in_=w1_rows[:, lo : lo + 2 * H])
 
         nc.vector.tensor_copy(out=xs_picked[:], in_=xs_table[:].indirect(offs_sb[:]))
         for r in range(4):
@@ -71,24 +71,20 @@ def tile_picked_phpair_relu_p_kernel(
         xw_picked = keep.tile([P, S], U32, name="xw_picked", tag="words", align_bytes=64)
         nc.vector.tensor_copy(out=xw_picked[:], in_=xw_table[:].indirect(offs_sb[:]))
 
-        w1_src = [raw[:].rearrange("p j (m t) -> p m t j", t=PACK) for raw in w1_raw]
-        stage_at = (3 * H // 2, 5 * H // 2, 0, H)
-
-        def round_w1(a, t0, t1, engine, m0=0, m1=P):
-            at = stage_at[t0]
-            staged = w1_bf[:, at : at + H * (t1 - t0)].rearrange("p (s m j) -> p m s j", s=t1 - t0, j=PACK)
-            dst, src = staged[:, m0:m1, :, 2 * a : 2 * a + 2], w1_src[a][:, m0:m1, t0:t1, :]
+        def round_w1(j0, j1, t0, t1, m0, m1, engine):
+            rows = w1_raw[:, H * j0 : H * j1].rearrange("p (j m t) -> p m t j", j=j1 - j0, t=PACK)
+            staged = w1_bf[:, H * t0 : H * t1].rearrange("p (t m j) -> p m t j", t=t1 - t0, j=PACK)
+            dst, src = staged[:, m0:m1, :, j0:j1], rows[:, m0:m1, t0:t1, :]
             if engine == "vector":
                 nc.vector.tensor_copy(out=dst, in_=src)
             else:
                 nc.scalar.activation(out=dst, in_=src, func=ACT.Copy)
 
         def quantise_w1(t0, t1):
-            at = stage_at[t0]
             nc.vector.quantize_mx(
                 out=w1_codes[:, P * t0 : P * t1].bitcast(FP8X4),
                 scales=w1_plane[:, P * t0 : P * t1],
-                in_=w1_bf[:, at : at + H * (t1 - t0)],
+                in_=w1_bf[:, H * t0 : H * t1],
             )
 
         h_sb = [keep.tile([P, S], F32, name="h_sb%d" % t, align_bytes=64) for t in range(PACK)]
@@ -109,15 +105,14 @@ def tile_picked_phpair_relu_p_kernel(
             else:
                 nc.scalar.copy(out=h_sb[t][:, lo : lo + width], in_=acc[:, 0:width])
 
-        round_w1(0, 0, 2, "scalar")
-        round_w1(1, 0, 1, "scalar", 0, P // 2)
-        round_w1(1, 0, 1, "vector", P // 2, P)
+        round_w1(0, 2, 0, 1, 0, P, "scalar")
+        round_w1(2, 4, 0, 1, 0, P // 2, "scalar")
+        round_w1(2, 4, 0, 1, P // 2, P, "vector")
         quantise_w1(0, 1)
-        round_w1(1, 1, 2, "scalar")
-        round_w1(0, 2, 4, "vector")
-        round_w1(1, 2, 4, "vector")
-        quantise_w1(1, 2)
-        quantise_w1(2, 4)
+        for m in range(0, P, P // 4):
+            round_w1(0, 4, 1, 4, m, m + P // 4, "vector")
+        quantise_w1(1, 3)
+        quantise_w1(3, 4)
         project(0, 0, 256, "scalar")
         project(0, 256, 256, "scalar")
         project(0, 512, 256, "scalar")

@@ -18,8 +18,18 @@ ACT = mybir.ActivationFunctionType
 
 P = 128
 PACK = 4
+LIST_ROWS = 16
+BANK = 512
 X_EARLY = 384
-PAIR_CHUNKS = (256, 128, 128)
+FIRST_TILE = (
+    (0, 256, "scalar"),
+    (256, 256, "scalar"),
+    (512, 256, "scalar"),
+    (768, 128, "vector"),
+    (896, 128, "scalar"),
+)
+CHUNKS = ((256, 256), (0, 128), (128, 128))
+HALF_V = V // 2
 
 
 def tile_picked_phpair_relu_p_kernel(
@@ -32,16 +42,16 @@ def tile_picked_phpair_relu_p_kernel(
         psum = ctx.enter_context(tc.psum_pool(name="psum", bufs=7))
         psum_out = ctx.enter_context(tc.psum_pool(name="psum_out", bufs=1))
 
-        offs_sb = lists.tile([P, S // 16], U16, name="offs_sb")
-        left_sb = lists.tile([P, V // 16], U16, name="left_sb")
-        right_sb = lists.tile([P, V // 16], U16, name="right_sb")
+        offs_sb = lists.tile([P, S // LIST_ROWS], U16, name="offs_sb")
+        left_sb = lists.tile([P, V // LIST_ROWS], U16, name="left_sb")
+        right_sb = lists.tile([P, V // LIST_ROWS], U16, name="right_sb")
 
         xs_table = keep.tile([P, T], U8, name="xs_table", align_bytes=64)
         xs_picked = keep.tile([P, S], U8, name="xs_picked", align_bytes=64)
         xs_plane = keep.tile([P, S], U8, name="xs_plane", tag="plane", align_bytes=64)
         xw_table = keep.tile([P, T], U32, name="xw_table", align_bytes=64)
         w1_raw = keep.tile([P, PACK * H], F32, name="w1_raw", align_bytes=64)
-        w1_bf = keep.tile([P, PACK * H], BF16, name="w1_bf", align_bytes=64)
+        w1_bf = keep.tile([P, 3 * H], BF16, name="w1_bf", align_bytes=64)
         w1_codes = keep.tile([P, H], U32, name="w1_codes", align_bytes=64)
         w1_plane = keep.tile([P, H], U8, name="w1_plane", align_bytes=64)
 
@@ -71,10 +81,14 @@ def tile_picked_phpair_relu_p_kernel(
         xw_picked = keep.tile([P, S], U32, name="xw_picked", tag="words", align_bytes=64)
         nc.vector.tensor_copy(out=xw_picked[:], in_=xw_table[:].indirect(offs_sb[:]))
 
-        def round_w1(j0, j1, t0, t1, m0, m1, engine):
+        def staged_w1(t0, t1):
+            at = H * ((t0 - 1) % 3)
+            return w1_bf[:, at : at + H * (t1 - t0)]
+
+        def round_w1(j0, j1, t0, t1, engine):
             rows = w1_raw[:, H * j0 : H * j1].rearrange("p (j m t) -> p m t j", j=j1 - j0, t=PACK)
-            staged = w1_bf[:, H * t0 : H * t1].rearrange("p (t m j) -> p m t j", t=t1 - t0, j=PACK)
-            dst, src = staged[:, m0:m1, :, j0:j1], rows[:, m0:m1, t0:t1, :]
+            words = staged_w1(t0, t1).rearrange("p (t m j) -> p m t j", t=t1 - t0, j=PACK)
+            dst, src = words[:, :, :, j0:j1], rows[:, :, t0:t1, :]
             if engine == "vector":
                 nc.vector.tensor_copy(out=dst, in_=src)
             else:
@@ -84,13 +98,13 @@ def tile_picked_phpair_relu_p_kernel(
             nc.vector.quantize_mx(
                 out=w1_codes[:, P * t0 : P * t1].bitcast(FP8X4),
                 scales=w1_plane[:, P * t0 : P * t1],
-                in_=w1_bf[:, H * t0 : H * t1],
+                in_=staged_w1(t0, t1),
             )
 
         h_sb = [keep.tile([P, S], F32, name="h_sb%d" % t, align_bytes=64) for t in range(PACK)]
 
         def project(t, lo, width, engine):
-            acc = psum.tile([P, 512], F32, name="acc")
+            acc = psum.tile([P, BANK], F32, name="acc")
             nc.tensor.matmul_mx(
                 out=acc[:, 0:width],
                 lhsT=w1_codes[:, P * t : P * (t + 1)].bitcast(FP8X4),
@@ -105,22 +119,18 @@ def tile_picked_phpair_relu_p_kernel(
             else:
                 nc.scalar.copy(out=h_sb[t][:, lo : lo + width], in_=acc[:, 0:width])
 
-        round_w1(0, 2, 0, 1, 0, P, "scalar")
-        round_w1(2, 4, 0, 1, 0, P // 2, "scalar")
-        round_w1(2, 4, 0, 1, P // 2, P, "vector")
+        round_w1(0, 2, 0, 1, "scalar")
+        round_w1(2, 4, 0, 1, "scalar")
         quantise_w1(0, 1)
-        for m in range(0, P, P // 4):
-            round_w1(0, 4, 1, 4, m, m + P // 4, "vector")
-        quantise_w1(1, 3)
-        quantise_w1(3, 4)
-        project(0, 0, 256, "scalar")
-        project(0, 256, 256, "scalar")
-        project(0, 512, 256, "scalar")
-        project(0, 768, 128, "vector")
-        project(0, 896, 128, "scalar")
-        for t in (1, 2, 3):
-            for lo in (0, 512):
-                project(t, lo, 512, "scalar")
+        round_w1(0, 4, 1, 2, "scalar")
+        round_w1(0, 4, 2, 4, "vector")
+        quantise_w1(1, 2)
+        quantise_w1(2, 4)
+        for lo, width, engine in FIRST_TILE:
+            project(0, lo, width, engine)
+        for t in range(1, PACK):
+            for lo in range(0, S, BANK):
+                project(t, lo, BANK, "scalar")
 
         w2_codes = keep.tile([P, 2 * N], U8, name="w2_codes", tag="words", align_bytes=64)
         w2_plane = keep.tile([P, N], U8, name="w2_plane", tag="plane", align_bytes=64)
@@ -132,50 +142,46 @@ def tile_picked_phpair_relu_p_kernel(
                 in_=w2_scales[0, 4 * q : 4 * q + 4, :].bitcast(I32),
             )
 
-        starts = [256, 0, 128]
-        first = keep.tile([P, 1152], F32, name="diff_first", align_bytes=64)
-        second = keep.tile([P, 512], F32, name="diff_second", align_bytes=64)
-        right_first = [keep.tile([P, 256], F32, name="right_first%d" % t, align_bytes=64)[:] for t in range(3)]
-        right_first.append(second[:, 64:320])
-        right_rest = [keep.tile([P, 256], F32, name="right_rest%d" % t, align_bytes=64)[:] for t in range(PACK)]
-        first_diff = first[:, 0:1024].rearrange("p (t v) -> p t v", t=PACK)
-        second_diff = second[:].rearrange("p (t v) -> p t v", t=PACK)
-        third_low = first[:, 512:768].rearrange("p (t v) -> p t v", t=2)
-        third_high = first[:, 896:1152].rearrange("p (t v) -> p t v", t=2)
+        diff_a = keep.tile([P, 1152], F32, name="diff_a", align_bytes=64)
+        diff_b = keep.tile([P, 512], F32, name="diff_b", align_bytes=64)
+        right_upper = [keep.tile([P, HALF_V], F32, name="right_upper%d" % t, align_bytes=64)[:] for t in range(3)]
+        right_upper.append(diff_b[:, 64:320])
+        right_lower = [keep.tile([P, HALF_V], F32, name="right_lower%d" % t, align_bytes=64)[:] for t in range(PACK)]
+        diff0 = diff_a[:, 0:1024].rearrange("p (t v) -> p t v", t=PACK)
+        diff1 = diff_b[:].rearrange("p (t v) -> p t v", t=PACK)
+        diff2_low = diff_a[:, 512:768].rearrange("p (t v) -> p t v", t=2)
+        diff2_high = diff_a[:, 896:1152].rearrange("p (t v) -> p t v", t=2)
         diff = [
-            [first_diff[:, t, :] for t in range(PACK)],
-            [second_diff[:, t, :] for t in range(PACK)],
-            [third_low[:, 0, :], third_low[:, 1, :], third_high[:, 0, :], third_high[:, 1, :]],
+            [diff0[:, t, :] for t in range(PACK)],
+            [diff1[:, t, :] for t in range(PACK)],
+            [diff2_low[:, 0, :], diff2_low[:, 1, :], diff2_high[:, 0, :], diff2_high[:, 1, :]],
         ]
-        z_bf = [
-            keep.tile([P, PACK * n], BF16, name="z_bf%d" % c, align_bytes=64)[:] for c, n in enumerate(PAIR_CHUNKS)
-        ]
+        z_bf = [keep.tile([P, PACK * n], BF16, name="z_bf%d" % c, align_bytes=64)[:] for c, (lo, n) in enumerate(CHUNKS)]
 
         def fetch_right(t):
-            for lo, picked in ((256, right_first[t]), (0, right_rest[t])):
-                nc.vector.tensor_copy(
-                    out=picked, in_=h_sb[t][:].indirect(right_sb[:, lo // 16 : (lo + 256) // 16])
-                )
+            for lo, picked in ((HALF_V, right_upper[t]), (0, right_lower[t])):
+                offsets = right_sb[:, lo // LIST_ROWS : (lo + HALF_V) // LIST_ROWS]
+                nc.vector.tensor_copy(out=picked, in_=h_sb[t][:].indirect(offsets))
 
         def fetch_left(t, c):
-            lo, n = starts[c], PAIR_CHUNKS[c]
+            lo, n = CHUNKS[c]
             nc.vector.tensor_tensor(
                 out=diff[c][t],
-                in0=h_sb[t][:].indirect(left_sb[:, lo // 16 : (lo + n) // 16]),
-                in1=right_first[t] if c == 0 else right_rest[t][:, lo : lo + n],
+                in0=h_sb[t][:].indirect(left_sb[:, lo // LIST_ROWS : (lo + n) // LIST_ROWS]),
+                in1=right_upper[t] if c == 0 else right_lower[t][:, lo : lo + n],
                 op=ALU.subtract,
             )
 
-        def rectify(c, planes, t0, t1, engine):
+        def rectify(c, runs, t0, t1, engine):
             dst = z_bf[c].rearrange("p (a i t) -> p a t i", i=4, t=PACK)[:, :, t0:t1, :]
-            src = planes.rearrange("p t (a i) -> p a t i", i=4)
+            src = runs.rearrange("p t (a i) -> p a t i", i=4)
             if engine == "vector":
                 nc.vector.tensor_scalar(out=dst, in0=src, scalar1=0.0, scalar2=None, op0=ALU.max)
             else:
                 nc.scalar.activation(out=dst, in_=src, func=ACT.Relu)
 
         def second_layer(c):
-            lo, n = starts[c], PAIR_CHUNKS[c]
+            lo, n = CHUNKS[c]
             z_codes = keep.tile([P, n], U32, name="z_codes%d" % c, align_bytes=64)
             z_plane = keep.tile([P, n], U8, name="z_plane%d" % c, align_bytes=64)
             nc.vector.quantize_mx(
@@ -195,7 +201,7 @@ def tile_picked_phpair_relu_p_kernel(
                     stop=True,
                 )
 
-            if c < len(PAIR_CHUNKS) - 1:
+            if c < len(CHUNKS) - 1:
                 acc = (psum if c else psum_out).tile([P, 2, n], F32, name="acc")
                 for half in range(2):
                     multiply(half, acc[:, half, :])
@@ -220,16 +226,16 @@ def tile_picked_phpair_relu_p_kernel(
             fetch_right(t)
             fetch_left(t, 0)
             if t % 2:
-                rectify(0, first_diff[:, t - 1 : t + 1, :], t - 1, t + 1, "scalar")
+                rectify(0, diff0[:, t - 1 : t + 1, :], t - 1, t + 1, "scalar")
         for t in (3, 0, 1, 2):
             fetch_left(t, 1)
-        rectify(1, second_diff, 0, 4, "scalar")
+        rectify(1, diff1, 0, PACK, "scalar")
         fetch_left(3, 2)
         second_layer(0)
         fetch_left(2, 2)
-        rectify(2, third_high, 2, 4, "scalar")
+        rectify(2, diff2_high, 2, PACK, "scalar")
         fetch_left(0, 2)
         fetch_left(1, 2)
         second_layer(1)
-        rectify(2, third_low, 0, 2, "vector")
+        rectify(2, diff2_low, 0, 2, "vector")
         second_layer(2)

@@ -64,13 +64,13 @@ def tile_picked_phpair_relu_p_kernel(
         x_rows = x_words[0].rearrange("p c r -> p (c r)").bitcast(I32)
         nc.sync.dma_start(offs_sb[:], offs)
         nc.sync.dma_start(out=xw_table[:, 0:X_EARLY].bitcast(I32), in_=x_rows[:, 0:X_EARLY])
-        nc.sync.dma_start(left_sb[:], left)
-        nc.sync.dma_start(right_sb[:], right)
         nc.sync.dma_start(out=xs_table[0:P:8, :].bitcast(I32), in_=x_scales[0].bitcast(I32))
         nc.sync.dma_start(out=xw_table[:, X_EARLY:T].bitcast(I32), in_=x_rows[:, X_EARLY:T])
         w1_rows = w1.rearrange("(p j) c -> p (j c)", j=PACK)
         for lo in (0, 2 * H):
             nc.sync.dma_start(out=w1_raw[:, lo : lo + 2 * H], in_=w1_rows[:, lo : lo + 2 * H])
+        nc.sync.dma_start(right_sb[:], right)
+        nc.sync.dma_start(left_sb[:], left)
 
         nc.vector.tensor_copy(out=xs_picked[:], in_=xs_table[:].indirect(offs_sb[:]))
         for r in range(4):

@@ -20,7 +20,7 @@ P = 128
 PACK = 4
 LIST_ROWS = 16
 BANK = 512
-X_EARLY = 384
+X_EARLY = 512
 FIRST_TILE = (
     (0, 256, "scalar"),
     (256, 256, "scalar"),
@@ -28,8 +28,8 @@ FIRST_TILE = (
     (768, 128, "vector"),
     (896, 128, "scalar"),
 )
-CHUNKS = ((256, 256), (0, 128), (128, 128))
-HALF_V = V // 2
+CHUNKS = ((256, 256), (128, 128), (0, 128))
+LOW = 128
 
 
 def tile_picked_phpair_relu_p_kernel(
@@ -62,8 +62,8 @@ def tile_picked_phpair_relu_p_kernel(
         nc.vector.memset(xs_plane[:].bitcast(I32), 0)
 
         x_rows = x_words[0].rearrange("p c r -> p (c r)").bitcast(I32)
-        nc.sync.dma_start(offs_sb[:], offs)
         nc.sync.dma_start(out=xw_table[:, 0:X_EARLY].bitcast(I32), in_=x_rows[:, 0:X_EARLY])
+        nc.sync.dma_start(offs_sb[:], offs)
         nc.sync.dma_start(out=xs_table[0:P:8, :].bitcast(I32), in_=x_scales[0].bitcast(I32))
         nc.sync.dma_start(out=xw_table[:, X_EARLY:T].bitcast(I32), in_=x_rows[:, X_EARLY:T])
         w1_rows = w1.rearrange("(p j) c -> p (j c)", j=PACK)
@@ -142,43 +142,50 @@ def tile_picked_phpair_relu_p_kernel(
                 in_=w2_scales[0, 4 * q : 4 * q + 4, :].bitcast(I32),
             )
 
-        diff_a = keep.tile([P, 1152], F32, name="diff_a", align_bytes=64)
-        diff_b = keep.tile([P, 512], F32, name="diff_b", align_bytes=64)
-        right_upper = [keep.tile([P, HALF_V], F32, name="right_upper%d" % t, align_bytes=64)[:] for t in range(3)]
-        right_upper.append(diff_b[:, 64:320])
-        right_lower = [keep.tile([P, HALF_V], F32, name="right_lower%d" % t, align_bytes=64)[:] for t in range(PACK)]
-        diff0 = diff_a[:, 0:1024].rearrange("p (t v) -> p t v", t=PACK)
-        diff1 = diff_b[:].rearrange("p (t v) -> p t v", t=PACK)
-        diff2_low = diff_a[:, 512:768].rearrange("p (t v) -> p t v", t=2)
-        diff2_high = diff_a[:, 896:1152].rearrange("p (t v) -> p t v", t=2)
-        diff = [
-            [diff0[:, t, :] for t in range(PACK)],
-            [diff1[:, t, :] for t in range(PACK)],
-            [diff2_low[:, 0, :], diff2_low[:, 1, :], diff2_high[:, 0, :], diff2_high[:, 1, :]],
-        ]
+        upper = V - LOW
+        diff_low = keep.tile([P, 2, upper], F32, name="diff_low", align_bytes=64)
+        diff_high = keep.tile([P, 512], F32, name="diff_high", align_bytes=64)
+        ends = keep.tile([P, 640], F32, name="ends", align_bytes=64)
+        right_upper = [keep.tile([P, upper], F32, name="right_upper%d" % t, align_bytes=64)[:] for t in range(3)]
+        right_upper.append(ends[:, 0:upper])
+        right_lower = [keep.tile([P, LOW], F32, name="right_lower%d" % t, align_bytes=64)[:] for t in range(PACK)]
+        late_high = ends[:, 128:640].rearrange("p (t v) -> p t v", t=2)
+        runs = {
+            (0, 0): diff_low[:, :, 128:384],
+            (0, 2): diff_high[:].rearrange("p (t v) -> p t v", t=2),
+            (1, 0): diff_low[:, :, 0:128],
+            (1, 2): late_high[:, :, 0:128],
+            (2, 0): diff_high[:, 0:256].rearrange("p (t v) -> p t v", t=2),
+            (2, 2): late_high[:, :, 128:256],
+        }
         z_bf = [keep.tile([P, PACK * n], BF16, name="z_bf%d" % c, align_bytes=64)[:] for c, (lo, n) in enumerate(CHUNKS)]
 
         def fetch_right(t):
-            for lo, picked in ((HALF_V, right_upper[t]), (0, right_lower[t])):
-                offsets = right_sb[:, lo // LIST_ROWS : (lo + HALF_V) // LIST_ROWS]
+            for lo, hi, picked in ((LOW, V, right_upper[t]), (0, LOW, right_lower[t])):
+                offsets = right_sb[:, lo // LIST_ROWS : hi // LIST_ROWS]
                 nc.vector.tensor_copy(out=picked, in_=h_sb[t][:].indirect(offsets))
 
-        def fetch_left(t, c):
-            lo, n = CHUNKS[c]
+        def subtract(t, lo, n, dst):
             nc.vector.tensor_tensor(
-                out=diff[c][t],
+                out=dst,
                 in0=h_sb[t][:].indirect(left_sb[:, lo // LIST_ROWS : (lo + n) // LIST_ROWS]),
-                in1=right_upper[t] if c == 0 else right_lower[t][:, lo : lo + n],
+                in1=right_lower[t] if lo < LOW else right_upper[t][:, lo - LOW : lo - LOW + n],
                 op=ALU.subtract,
             )
 
-        def rectify(c, runs, t0, t1, engine):
-            dst = z_bf[c].rearrange("p (a i t) -> p a t i", i=4, t=PACK)[:, :, t0:t1, :]
-            src = runs.rearrange("p t (a i) -> p a t i", i=4)
+        def fetch_left(t, c):
+            lo, n = CHUNKS[c]
+            subtract(t, lo, n, runs[c, t - t % 2][:, t % 2, :])
+
+        def rectify(c, t0, engine):
+            dst = z_bf[c].rearrange("p (a i t) -> p a t i", i=4, t=PACK)[:, :, t0 : t0 + 2, :]
+            src = runs[c, t0].rearrange("p t (a i) -> p a t i", i=4)
             if engine == "vector":
                 nc.vector.tensor_scalar(out=dst, in0=src, scalar1=0.0, scalar2=None, op0=ALU.max)
             else:
                 nc.scalar.activation(out=dst, in_=src, func=ACT.Relu)
+
+        copies, stores = [], []
 
         def second_layer(c):
             lo, n = CHUNKS[c]
@@ -201,41 +208,46 @@ def tile_picked_phpair_relu_p_kernel(
                     stop=True,
                 )
 
-            if c < len(CHUNKS) - 1:
-                acc = (psum if c else psum_out).tile([P, 2, n], F32, name="acc")
+            if c == 1:
+                acc = psum.tile([P, 2, n], F32, name="acc")
                 for half in range(2):
                     multiply(half, acc[:, half, :])
-                result = keep.tile([P, 2, n], F32, name="result%d" % c, align_bytes=64)
-                nc.scalar.copy(out=result[:], in_=acc[:])
-                (nc.scalar if c else nc.sync).dma_start(
-                    out=out[:, lo : lo + n].rearrange("(a p) v -> p a v", p=P), in_=result[:]
-                )
+                result = keep.tile([P, 2, n], F32, name="result1", align_bytes=64)
+                copies.append((result, acc))
+                stores.append((out[:, lo : lo + n].rearrange("(a p) v -> p a v", p=P), result))
             else:
+                for result, acc in copies:
+                    nc.vector.tensor_copy(out=result[:], in_=acc[:])
+                for dst, result in stores:
+                    nc.scalar.dma_start(out=dst, in_=result[:])
                 for half in range(2):
                     acc = (psum_out if half else psum).tile([P, n], F32, name="acc")
                     multiply(half, acc[:])
-                    result = keep.tile([P, n], F32, name="last%d" % half, align_bytes=64)
-                    if half == 0:
+                    result = keep.tile([P, n], F32, name="result%d_%d" % (c, half), align_bytes=64)
+                    if c == 0:
                         nc.scalar.copy(out=result[:], in_=acc[:])
-                        nc.scalar.dma_start(out=out[0:P, lo : lo + n], in_=result[:])
                     else:
                         nc.vector.tensor_copy(out=result[:], in_=acc[:])
-                        nc.sync.dma_start(out=out[P : 2 * P, lo : lo + n], in_=result[:])
+                    (nc.scalar if c == 2 and half == 0 else nc.sync).dma_start(
+                        out=out[P * half : P * (half + 1), lo : lo + n], in_=result[:]
+                    )
 
-        for t in range(PACK):
+        for t in range(2):
+            fetch_right(t)
+            subtract(t, LOW, upper, diff_low[:, t, :])
+        rectify(0, 0, "scalar")
+        rectify(1, 0, "scalar")
+        for t in range(2, PACK):
             fetch_right(t)
             fetch_left(t, 0)
-            if t % 2:
-                rectify(0, diff0[:, t - 1 : t + 1, :], t - 1, t + 1, "scalar")
-        for t in (3, 0, 1, 2):
-            fetch_left(t, 1)
-        rectify(1, diff1, 0, PACK, "scalar")
-        fetch_left(3, 2)
+        rectify(0, 2, "scalar")
+        for c in (1, 2):
+            fetch_left(3, c)
+            fetch_left(2, c)
+            rectify(c, 2, "scalar")
         second_layer(0)
-        fetch_left(2, 2)
-        rectify(2, diff2_high, 2, PACK, "scalar")
         fetch_left(0, 2)
         fetch_left(1, 2)
         second_layer(1)
-        rectify(2, diff2_low, 0, 2, "vector")
+        rectify(2, 0, "vector")
         second_layer(2)

@@ -48,7 +48,7 @@ def tile_picked_phpair_relu_p_kernel(
 
         xs_table = keep.tile([P, T], U8, name="xs_table", align_bytes=64)
         xs_picked = keep.tile([P, S], U8, name="xs_picked", align_bytes=64)
-        xs_plane = keep.tile([P, S], U8, name="xs_plane", tag="plane", align_bytes=64)
+        xs_plane = keep.tile([P, S], U8, name="xs_plane", align_bytes=64)
         xw_table = keep.tile([P, T], U32, name="xw_table", align_bytes=64)
         w1_raw = keep.tile([P, PACK * H], F32, name="w1_raw", align_bytes=64)
         w1_bf = keep.tile([P, 3 * H], BF16, name="w1_bf", align_bytes=64)
@@ -74,7 +74,7 @@ def tile_picked_phpair_relu_p_kernel(
 
         nc.vector.tensor_copy(out=xs_picked[:], in_=xs_table[:].indirect(offs_sb[:]))
         for r in range(4):
-            nc.scalar.dma_start(
+            (nc.sync if r % 2 else nc.scalar).dma_start(
                 out=xs_plane[r:P:32, :].bitcast(I32), in_=xs_picked[8 * r : P : 32, :].bitcast(I32)
             )
 
@@ -133,8 +133,7 @@ def tile_picked_phpair_relu_p_kernel(
                 project(t, lo, BANK, "scalar")
 
         w2_codes = keep.tile([P, 2 * N], U8, name="w2_codes", tag="words", align_bytes=64)
-        w2_plane = keep.tile([P, N], U8, name="w2_plane", tag="plane", align_bytes=64)
-        nc.gpsimd.memset(w2_plane[:].bitcast(I32), 0)
+        w2_plane = w1_plane[:, H - N : H]
         nc.sync.dma_start(out=w2_codes[:].bitcast(I32), in_=w2_words[0].bitcast(I32))
         for q in range(4):
             nc.sync.dma_start(
@@ -143,33 +142,32 @@ def tile_picked_phpair_relu_p_kernel(
             )
 
         upper = V - LOW
-        diff_low = keep.tile([P, 2, upper], F32, name="diff_low", align_bytes=64)
-        diff_high = keep.tile([P, 512], F32, name="diff_high", align_bytes=64)
-        ends = keep.tile([P, 640], F32, name="ends", align_bytes=64)
-        right_upper = [keep.tile([P, upper], F32, name="right_upper%d" % t, align_bytes=64)[:] for t in range(3)]
-        right_upper.append(ends[:, 0:upper])
-        right_lower = [keep.tile([P, LOW], F32, name="right_lower%d" % t, align_bytes=64)[:] for t in range(PACK)]
-        late_high = ends[:, 128:640].rearrange("p (t v) -> p t v", t=2)
+        work = keep.tile([P, 6 * V], F32, name="work", align_bytes=64)
+        ends = work[:, 0 : 2 * V]
+        diff_low = work[:, 2 * V : 2 * V + 2 * upper].rearrange("p (t v) -> p t v", t=2)
+        rights = [keep.tile([P, V], F32, name="right%d" % t, align_bytes=64)[:] for t in range(2)]
+        rights.extend([ends[:, V : 2 * V], ends[:, 0:V]])
+        late_high = ends.rearrange("p (t v) -> p t v", t=2)[:, :, 256:512]
         runs = {
             (0, 0): diff_low[:, :, 128:384],
-            (0, 2): diff_high[:].rearrange("p (t v) -> p t v", t=2),
+            (0, 2): diff_low[:, :, 128:384],
             (1, 0): diff_low[:, :, 0:128],
-            (1, 2): late_high[:, :, 0:128],
-            (2, 0): diff_high[:, 0:256].rearrange("p (t v) -> p t v", t=2),
-            (2, 2): late_high[:, :, 128:256],
+            (1, 2): late_high[:, :, 128:256],
+            (2, 0): work[:].rearrange("p (t v) -> p t v", t=2)[:, :, 0:128],
+            (2, 2): late_high[:, :, 0:128],
         }
         z_bf = [keep.tile([P, PACK * n], BF16, name="z_bf%d" % c, align_bytes=64)[:] for c, (lo, n) in enumerate(CHUNKS)]
 
-        def fetch_right(t):
-            for lo, hi, picked in ((LOW, V, right_upper[t]), (0, LOW, right_lower[t])):
+        def fetch_right(t, cuts):
+            for lo, hi in cuts:
                 offsets = right_sb[:, lo // LIST_ROWS : hi // LIST_ROWS]
-                nc.vector.tensor_copy(out=picked, in_=h_sb[t][:].indirect(offsets))
+                nc.vector.tensor_copy(out=rights[t][:, lo:hi], in_=h_sb[t][:].indirect(offsets))
 
         def subtract(t, lo, n, dst):
             nc.vector.tensor_tensor(
                 out=dst,
                 in0=h_sb[t][:].indirect(left_sb[:, lo // LIST_ROWS : (lo + n) // LIST_ROWS]),
-                in1=right_lower[t] if lo < LOW else right_upper[t][:, lo - LOW : lo - LOW + n],
+                in1=rights[t][:, lo : lo + n],
                 op=ALU.subtract,
             )
 
@@ -185,7 +183,7 @@ def tile_picked_phpair_relu_p_kernel(
             else:
                 nc.scalar.activation(out=dst, in_=src, func=ACT.Relu)
 
-        copies, stores = [], []
+        waiting = []
 
         def second_layer(c):
             lo, n = CHUNKS[c]
@@ -212,13 +210,11 @@ def tile_picked_phpair_relu_p_kernel(
                 acc = psum.tile([P, 2, n], F32, name="acc")
                 for half in range(2):
                     multiply(half, acc[:, half, :])
-                result = keep.tile([P, 2, n], F32, name="result1", align_bytes=64)
-                copies.append((result, acc))
-                stores.append((out[:, lo : lo + n].rearrange("(a p) v -> p a v", p=P), result))
+                waiting.append((acc, out[:, lo : lo + n].rearrange("(a p) v -> p a v", p=P)))
             else:
-                for result, acc in copies:
+                for acc, dst in waiting:
+                    result = keep.tile([P, 2, n], F32, name="result1", tag="z_bf2", align_bytes=64)
                     nc.vector.tensor_copy(out=result[:], in_=acc[:])
-                for dst, result in stores:
                     nc.scalar.dma_start(out=dst, in_=result[:])
                 for half in range(2):
                     acc = (psum_out if half else psum).tile([P, n], F32, name="acc")
@@ -233,20 +229,21 @@ def tile_picked_phpair_relu_p_kernel(
                     )
 
         for t in range(2):
-            fetch_right(t)
+            fetch_right(t, ((LOW, V), (0, LOW)))
             subtract(t, LOW, upper, diff_low[:, t, :])
         rectify(0, 0, "scalar")
         rectify(1, 0, "scalar")
         for t in range(2, PACK):
-            fetch_right(t)
+            fetch_right(t, ((0, V),))
+        for t in range(2, PACK):
             fetch_left(t, 0)
         rectify(0, 2, "scalar")
-        for c in (1, 2):
-            fetch_left(3, c)
-            fetch_left(2, c)
-            rectify(c, 2, "scalar")
-        second_layer(0)
+        for t in (3, 2):
+            subtract(t, 0, 256, late_high[:, t - 2, :])
+        rectify(1, 2, "scalar")
+        rectify(2, 2, "scalar")
         fetch_left(0, 2)
+        second_layer(0)
         fetch_left(1, 2)
         second_layer(1)
         rectify(2, 0, "vector")

@@ -229,8 +229,13 @@ def tile_picked_phpair_relu_p_kernel(
                     )
 
         for t in range(2):
-            fetch_right(t, ((LOW, V), (0, LOW)))
-            subtract(t, LOW, upper, diff_low[:, t, :])
+            fetch_right(t, ((0, V),))
+            lefts = keep.tile([P, upper], F32, name="left%d" % t, align_bytes=64)
+            nc.vector.tensor_copy(out=lefts[:], in_=h_sb[t][:].indirect(left_sb[:, LOW // LIST_ROWS : V // LIST_ROWS]))
+            for lo, hi in ((128, upper), (0, 128)):
+                nc.gpsimd.tensor_tensor(
+                    out=diff_low[:, t, lo:hi], in0=lefts[:, lo:hi], in1=rights[t][:, LOW + lo : LOW + hi], op=ALU.subtract
+                )
         rectify(0, 0, "scalar")
         rectify(1, 0, "scalar")
         for t in range(2, PACK):

@@ -120,7 +120,12 @@ def tile_picked_phpair_relu_p_kernel(
                 nc.scalar.copy(out=h_sb[t][:, lo : lo + width], in_=acc[:, 0:width])
 
         round_w1(0, 2, 0, 1, "scalar")
-        round_w1(2, 4, 0, 1, "scalar")
+        rows = w1_raw[:, 2 * H : 4 * H].rearrange("p (j m t) -> p m t j", j=2, t=PACK)[:, :, 0, :]
+        words = staged_w1(0, 1).rearrange("p (m j) -> p m j", j=PACK)[:, :, 2:4]
+        nc.scalar.activation(out=words[:, 0:64, :], in_=rows[:, 0:64, :], func=ACT.Copy)
+        nc.gpsimd.tensor_scalar(
+            out=words[:, 64:P, :], in0=rows[:, 64:P, :], scalar1=1.0, scalar2=0.0, op0=ALU.mult, op1=ALU.add
+        )
         quantise_w1(0, 1)
         round_w1(0, 4, 1, 2, "scalar")
         round_w1(0, 4, 2, 4, "vector")

@@ -39,6 +39,7 @@ def tile_picked_phpair_relu_p_kernel(
     with ExitStack() as ctx:
         lists = ctx.enter_context(tc.tile_pool(name="lists", bufs=1))
         keep = ctx.enter_context(tc.tile_pool(name="keep", bufs=1))
+        turns = ctx.enter_context(tc.tile_pool(name="turns", bufs=1))
         psum = ctx.enter_context(tc.psum_pool(name="psum", bufs=7))
         psum_out = ctx.enter_context(tc.psum_pool(name="psum_out", bufs=1))
 
@@ -51,8 +52,13 @@ def tile_picked_phpair_relu_p_kernel(
         xs_plane = keep.tile([P, S], U8, name="xs_plane", align_bytes=64)
         xw_table = keep.tile([P, T], U32, name="xw_table", align_bytes=64)
         w1_raw = keep.tile([P, PACK * H], F32, name="w1_raw", align_bytes=64)
-        w1_bf = keep.tile([P, 3 * H], BF16, name="w1_bf", align_bytes=64)
+        staged = {
+            0: turns.tile([P, H], BF16, name="staged0", offset=0, align_bytes=64),
+            1: keep.tile([P, H], BF16, name="staged1", align_bytes=64),
+            2: turns.tile([P, 2 * H], BF16, name="staged2", offset=H, align_bytes=64),
+        }
         w1_codes = keep.tile([P, H], U32, name="w1_codes", align_bytes=64)
+        codes1 = turns.tile([P, P], U32, name="codes1", offset=0, align_bytes=64)
         w1_plane = keep.tile([P, H], U8, name="w1_plane", align_bytes=64)
 
         warm = keep.tile([P, 16], F32, name="warm", align_bytes=64)
@@ -82,8 +88,10 @@ def tile_picked_phpair_relu_p_kernel(
         nc.vector.tensor_copy(out=xw_picked[:], in_=xw_table[:].indirect(offs_sb[:]))
 
         def staged_w1(t0, t1):
-            at = H * ((t0 - 1) % 3)
-            return w1_bf[:, at : at + H * (t1 - t0)]
+            return staged[t0][:]
+
+        def codes_w1(t0, t1):
+            return codes1[:] if t0 == 1 else w1_codes[:, P * t0 : P * t1]
 
         def round_w1(j0, j1, t0, t1, engine):
             rows = w1_raw[:, H * j0 : H * j1].rearrange("p (j m t) -> p m t j", j=j1 - j0, t=PACK)
@@ -91,12 +99,14 @@ def tile_picked_phpair_relu_p_kernel(
             dst, src = words[:, :, :, j0:j1], rows[:, :, t0:t1, :]
             if engine == "vector":
                 nc.vector.tensor_copy(out=dst, in_=src)
+            elif engine == "gpsimd":
+                nc.gpsimd.tensor_scalar(out=dst, in0=src, scalar1=1.0, scalar2=0.0, op0=ALU.mult, op1=ALU.add)
             else:
                 nc.scalar.activation(out=dst, in_=src, func=ACT.Copy)
 
         def quantise_w1(t0, t1):
             nc.vector.quantize_mx(
-                out=w1_codes[:, P * t0 : P * t1].bitcast(FP8X4),
+                out=codes_w1(t0, t1).bitcast(FP8X4),
                 scales=w1_plane[:, P * t0 : P * t1],
                 in_=staged_w1(t0, t1),
             )
@@ -107,7 +117,7 @@ def tile_picked_phpair_relu_p_kernel(
             acc = psum.tile([P, BANK], F32, name="acc")
             nc.tensor.matmul_mx(
                 out=acc[:, 0:width],
-                lhsT=w1_codes[:, P * t : P * (t + 1)].bitcast(FP8X4),
+                lhsT=codes_w1(t, t + 1).bitcast(FP8X4),
                 lhsT_scale=w1_plane[:, P * t : P * (t + 1)],
                 rhs=xw_picked[:, lo : lo + width].bitcast(FP8X4),
                 rhs_scale=xs_plane[:, lo : lo + width],
@@ -120,6 +130,7 @@ def tile_picked_phpair_relu_p_kernel(
                 nc.scalar.copy(out=h_sb[t][:, lo : lo + width], in_=acc[:, 0:width])
 
         round_w1(0, 2, 0, 1, "scalar")
+        round_w1(0, 2, 1, 2, "gpsimd")
         rows = w1_raw[:, 2 * H : 4 * H].rearrange("p (j m t) -> p m t j", j=2, t=PACK)[:, :, 0, :]
         words = staged_w1(0, 1).rearrange("p (m j) -> p m j", j=PACK)[:, :, 2:4]
         nc.scalar.activation(out=words[:, 0:64, :], in_=rows[:, 0:64, :], func=ACT.Copy)
@@ -127,7 +138,7 @@ def tile_picked_phpair_relu_p_kernel(
             out=words[:, 64:P, :], in0=rows[:, 64:P, :], scalar1=1.0, scalar2=0.0, op0=ALU.mult, op1=ALU.add
         )
         quantise_w1(0, 1)
-        round_w1(0, 4, 1, 2, "scalar")
+        round_w1(2, 4, 1, 2, "scalar")
         round_w1(0, 4, 2, 4, "vector")
         quantise_w1(1, 2)
         quantise_w1(2, 4)

@@ -29,7 +29,6 @@ FIRST_TILE = (
     (896, 128, "scalar"),
 )
 CHUNKS = ((256, 256), (128, 128), (0, 128))
-LOW = 128
 
 
 def tile_picked_phpair_relu_p_kernel(
@@ -40,8 +39,9 @@ def tile_picked_phpair_relu_p_kernel(
         lists = ctx.enter_context(tc.tile_pool(name="lists", bufs=1))
         keep = ctx.enter_context(tc.tile_pool(name="keep", bufs=1))
         turns = ctx.enter_context(tc.tile_pool(name="turns", bufs=1))
-        psum = ctx.enter_context(tc.psum_pool(name="psum", bufs=7))
-        psum_out = ctx.enter_context(tc.psum_pool(name="psum_out", bufs=1))
+        zpool = ctx.enter_context(tc.tile_pool(name="zpool", bufs=1))
+        turns2 = ctx.enter_context(tc.tile_pool(name="turns2", bufs=1))
+        psum = ctx.enter_context(tc.psum_pool(name="psum", bufs=8))
 
         offs_sb = lists.tile([P, S // LIST_ROWS], U16, name="offs_sb")
         left_sb = lists.tile([P, V // LIST_ROWS], U16, name="left_sb")
@@ -57,7 +57,8 @@ def tile_picked_phpair_relu_p_kernel(
             1: keep.tile([P, H], BF16, name="staged1", align_bytes=64),
             2: turns.tile([P, 2 * H], BF16, name="staged2", offset=H, align_bytes=64),
         }
-        w1_codes = keep.tile([P, H], U32, name="w1_codes", align_bytes=64)
+        codes0 = keep.tile([P, P], U32, name="codes0", align_bytes=64)
+        codes23 = turns2.tile([P, 2 * P], U32, name="codes23", offset=0, align_bytes=64)
         codes1 = turns.tile([P, P], U32, name="codes1", offset=0, align_bytes=64)
         w1_plane = keep.tile([P, H], U8, name="w1_plane", align_bytes=64)
 
@@ -91,7 +92,9 @@ def tile_picked_phpair_relu_p_kernel(
             return staged[t0][:]
 
         def codes_w1(t0, t1):
-            return codes1[:] if t0 == 1 else w1_codes[:, P * t0 : P * t1]
+            if t0 >= 2:
+                return codes23[:, P * (t0 - 2) : P * (t1 - 2)]
+            return codes1[:] if t0 == 1 else codes0[:]
 
         def round_w1(j0, j1, t0, t1, engine):
             rows = w1_raw[:, H * j0 : H * j1].rearrange("p (j m t) -> p m t j", j=j1 - j0, t=PACK)
@@ -144,9 +147,42 @@ def tile_picked_phpair_relu_p_kernel(
         quantise_w1(2, 4)
         for lo, width, engine in FIRST_TILE:
             project(0, lo, width, engine)
-        for t in range(1, PACK):
+
+        rights = [keep.tile([P, V], F32, name="right%d" % t, align_bytes=64) for t in (0, 1)]
+        rights.append(keep.tile([P, V], F32, name="right2", align_bytes=64))
+        rights.append(keep.tile([P, V], F32, name="right3", align_bytes=64))
+        diffs = turns.tile([P, PACK, V], F32, name="diffs", offset=0, align_bytes=64)
+        z_bf = [
+            zpool.tile([P, PACK * 256], BF16, name="z_bf0", offset=0, align_bytes=64)[:],
+            keep.tile([P, PACK * 128], BF16, name="z_bf1", align_bytes=64)[:],
+            zpool.tile([P, PACK * 128], BF16, name="z_bf2", offset=0, align_bytes=64)[:],
+        ]
+
+        def fetch_right(t, lo, n):
+            offsets = right_sb[:, lo // LIST_ROWS : (lo + n) // LIST_ROWS]
+            nc.scalar.activation(out=rights[t][:, lo : lo + n], in_=h_sb[t][:].indirect(offsets), func=ACT.Copy)
+
+        def fetch_left(t, lo, n):
+            nc.vector.tensor_tensor(
+                out=diffs[:, t, lo : lo + n],
+                in0=h_sb[t][:].indirect(left_sb[:, lo // LIST_ROWS : (lo + n) // LIST_ROWS]),
+                in1=rights[t][:, lo : lo + n],
+                op=ALU.subtract,
+            )
+
+        def rectify(c, t0, t1, engine):
+            lo, n = CHUNKS[c]
+            dst = z_bf[c].rearrange("p (a i t) -> p a t i", i=4, t=PACK)[:, :, t0:t1, :]
+            src = diffs[:, t0:t1, lo : lo + n].rearrange("p t (a i) -> p a t i", i=4)
+            if engine == "vector":
+                nc.vector.tensor_scalar(out=dst, in0=src, scalar1=0.0, scalar2=None, op0=ALU.max)
+            else:
+                nc.scalar.activation(out=dst, in_=src, func=ACT.Relu)
+
+        fetch_right(0, 0, V)
+        for t, engine in ((1, "vector"), (2, "scalar"), (3, "vector")):
             for lo in range(0, S, BANK):
-                project(t, lo, BANK, "scalar")
+                project(t, lo, BANK, engine)
 
         w2_codes = keep.tile([P, 2 * N], U8, name="w2_codes", tag="words", align_bytes=64)
         w2_plane = w1_plane[:, H - N : H]
@@ -157,63 +193,16 @@ def tile_picked_phpair_relu_p_kernel(
                 in_=w2_scales[0, 4 * q : 4 * q + 4, :].bitcast(I32),
             )
 
-        upper = V - LOW
-        work = keep.tile([P, 6 * V], F32, name="work", align_bytes=64)
-        ends = work[:, 0 : 2 * V]
-        diff_low = work[:, 2 * V : 2 * V + 2 * upper].rearrange("p (t v) -> p t v", t=2)
-        rights = [keep.tile([P, V], F32, name="right%d" % t, align_bytes=64)[:] for t in range(2)]
-        rights.extend([ends[:, V : 2 * V], ends[:, 0:V]])
-        late_high = ends.rearrange("p (t v) -> p t v", t=2)[:, :, 256:512]
-        runs = {
-            (0, 0): diff_low[:, :, 128:384],
-            (0, 2): diff_low[:, :, 128:384],
-            (1, 0): diff_low[:, :, 0:128],
-            (1, 2): late_high[:, :, 128:256],
-            (2, 0): work[:].rearrange("p (t v) -> p t v", t=2)[:, :, 0:128],
-            (2, 2): late_high[:, :, 0:128],
-        }
-        z_bf = [keep.tile([P, PACK * n], BF16, name="z_bf%d" % c, align_bytes=64)[:] for c, (lo, n) in enumerate(CHUNKS)]
 
-        def fetch_right(t, cuts):
-            for lo, hi in cuts:
-                offsets = right_sb[:, lo // LIST_ROWS : hi // LIST_ROWS]
-                nc.vector.tensor_copy(out=rights[t][:, lo:hi], in_=h_sb[t][:].indirect(offsets))
-
-        def subtract(t, lo, n, dst):
-            nc.vector.tensor_tensor(
-                out=dst,
-                in0=h_sb[t][:].indirect(left_sb[:, lo // LIST_ROWS : (lo + n) // LIST_ROWS]),
-                in1=rights[t][:, lo : lo + n],
-                op=ALU.subtract,
-            )
-
-        def fetch_left(t, c):
-            lo, n = CHUNKS[c]
-            subtract(t, lo, n, runs[c, t - t % 2][:, t % 2, :])
-
-        def rectify(c, t0, engine):
-            dst = z_bf[c].rearrange("p (a i t) -> p a t i", i=4, t=PACK)[:, :, t0 : t0 + 2, :]
-            src = runs[c, t0].rearrange("p t (a i) -> p a t i", i=4)
-            if engine == "vector":
-                nc.vector.tensor_scalar(out=dst, in0=src, scalar1=0.0, scalar2=None, op0=ALU.max)
-            else:
-                nc.scalar.activation(out=dst, in_=src, func=ACT.Relu)
-
-        waiting = []
-
-        def second_layer(c):
+        def second_layer(c, engine):
             lo, n = CHUNKS[c]
             z_codes = keep.tile([P, n], U32, name="z_codes%d" % c, align_bytes=64)
             z_plane = keep.tile([P, n], U8, name="z_plane%d" % c, align_bytes=64)
-            nc.vector.quantize_mx(
-                out=z_codes[:].bitcast(FP8X4),
-                scales=z_plane[:],
-                in_=z_bf[c],
-            )
-
-            def multiply(half, acc):
+            nc.vector.quantize_mx(out=z_codes[:].bitcast(FP8X4), scales=z_plane[:], in_=z_bf[c])
+            acc = psum.tile([P, 2, n], F32, name="acc")
+            for half in range(2):
                 nc.tensor.matmul_mx(
-                    out=acc,
+                    out=acc[:, half, :],
                     lhsT=w2_codes[:, 2 * P * half : 2 * P * (half + 1)].bitcast(FP4X4),
                     lhsT_scale=w2_plane[:, P * half : P * (half + 1)],
                     rhs=z_codes[:].bitcast(FP8X4),
@@ -221,51 +210,28 @@ def tile_picked_phpair_relu_p_kernel(
                     start=True,
                     stop=True,
                 )
-
-            if c == 1:
-                acc = psum.tile([P, 2, n], F32, name="acc")
-                for half in range(2):
-                    multiply(half, acc[:, half, :])
-                waiting.append((acc, out[:, lo : lo + n].rearrange("(a p) v -> p a v", p=P)))
+            result = keep.tile([P, 2, n], F32, name="result%d" % c, align_bytes=64)
+            if engine == "vector":
+                nc.vector.tensor_copy(out=result[:], in_=acc[:])
             else:
-                for acc, dst in waiting:
-                    result = keep.tile([P, 2, n], F32, name="result1", tag="z_bf2", align_bytes=64)
-                    nc.vector.tensor_copy(out=result[:], in_=acc[:])
-                    nc.scalar.dma_start(out=dst, in_=result[:])
-                for half in range(2):
-                    acc = (psum_out if half else psum).tile([P, n], F32, name="acc")
-                    multiply(half, acc[:])
-                    result = keep.tile([P, n], F32, name="result%d_%d" % (c, half), align_bytes=64)
-                    if c == 0:
-                        nc.scalar.copy(out=result[:], in_=acc[:])
-                    else:
-                        nc.vector.tensor_copy(out=result[:], in_=acc[:])
-                    (nc.scalar if c == 2 and half == 0 else nc.sync).dma_start(
-                        out=out[P * half : P * (half + 1), lo : lo + n], in_=result[:]
-                    )
+                nc.scalar.copy(out=result[:], in_=acc[:])
+            (nc.scalar if c == 1 else nc.sync).dma_start(
+                out=out[:, lo : lo + n].rearrange("(a p) v -> p a v", p=P), in_=result[:]
+            )
 
-        for t in range(2):
-            fetch_right(t, ((0, V),))
-            lefts = keep.tile([P, upper], F32, name="left%d" % t, align_bytes=64)
-            nc.vector.tensor_copy(out=lefts[:], in_=h_sb[t][:].indirect(left_sb[:, LOW // LIST_ROWS : V // LIST_ROWS]))
-            for lo, hi in ((128, upper), (0, 128)):
-                nc.gpsimd.tensor_tensor(
-                    out=diff_low[:, t, lo:hi], in0=lefts[:, lo:hi], in1=rights[t][:, LOW + lo : LOW + hi], op=ALU.subtract
-                )
-        rectify(0, 0, "scalar")
-        rectify(1, 0, "scalar")
-        for t in range(2, PACK):
-            fetch_right(t, ((0, V),))
-        for t in range(2, PACK):
-            fetch_left(t, 0)
-        rectify(0, 2, "scalar")
-        for t in (3, 2):
-            subtract(t, 0, 256, late_high[:, t - 2, :])
-        rectify(1, 2, "scalar")
-        rectify(2, 2, "scalar")
-        fetch_left(0, 2)
-        second_layer(0)
-        fetch_left(1, 2)
-        second_layer(1)
-        rectify(2, 0, "vector")
-        second_layer(2)
+        fetch_left(0, 0, V)
+        for t in (1, 2, 3):
+            fetch_right(t, 256, 256)
+            fetch_left(t, 256, 256)
+        for t in (1, 2):
+            fetch_right(t, 0, 256)
+            fetch_left(t, 0, 256)
+        for lo in (128, 0):
+            fetch_right(3, lo, 128)
+            fetch_left(3, lo, 128)
+        rectify(0, 0, 4, "scalar")
+        rectify(1, 0, 4, "scalar")
+        second_layer(0, "scalar")
+        rectify(2, 0, 4, "vector")
+        second_layer(1, "scalar")
+        second_layer(2, "vector")

@@ -194,13 +194,14 @@ def tile_picked_phpair_relu_p_kernel(
             )
 
 
-        def second_layer(c, engine):
+        def second_layer(c, engines, queues):
             lo, n = CHUNKS[c]
             z_codes = keep.tile([P, n], U32, name="z_codes%d" % c, align_bytes=64)
             z_plane = keep.tile([P, n], U8, name="z_plane%d" % c, align_bytes=64)
             nc.vector.quantize_mx(out=z_codes[:].bitcast(FP8X4), scales=z_plane[:], in_=z_bf[c])
-            acc = psum.tile([P, 2, n], F32, name="acc")
             for half in range(2):
+                if half == 0 or len(engines) == 2:
+                    acc = psum.tile([P, 2, n], F32, name="acc")
                 nc.tensor.matmul_mx(
                     out=acc[:, half, :],
                     lhsT=w2_codes[:, 2 * P * half : 2 * P * (half + 1)].bitcast(FP4X4),
@@ -210,13 +211,20 @@ def tile_picked_phpair_relu_p_kernel(
                     start=True,
                     stop=True,
                 )
-            result = keep.tile([P, 2, n], F32, name="result%d" % c, align_bytes=64)
+                if len(engines) == 2:
+                    leave(c, half, half + 1, acc, engines[half], queues[half])
+            if len(engines) == 1:
+                leave(c, 0, 2, acc, engines[0], queues[0])
+
+        def leave(c, h0, h1, acc, engine, queue):
+            lo, n = CHUNKS[c]
+            result = keep.tile([P, h1 - h0, n], F32, name="result%d_%d" % (c, h0), align_bytes=64)
             if engine == "vector":
-                nc.vector.tensor_copy(out=result[:], in_=acc[:])
+                nc.vector.tensor_copy(out=result[:], in_=acc[:, h0:h1, :])
             else:
-                nc.scalar.copy(out=result[:], in_=acc[:])
-            (nc.scalar if c == 1 else nc.sync).dma_start(
-                out=out[:, lo : lo + n].rearrange("(a p) v -> p a v", p=P), in_=result[:]
+                nc.scalar.copy(out=result[:], in_=acc[:, h0:h1, :])
+            queue.dma_start(
+                out=out[P * h0 : P * h1, lo : lo + n].rearrange("(a p) v -> p a v", p=P), in_=result[:]
             )
 
         fetch_left(0, 0, V)
@@ -231,7 +239,7 @@ def tile_picked_phpair_relu_p_kernel(
             fetch_left(3, lo, 128)
         rectify(0, 0, 4, "scalar")
         rectify(1, 0, 4, "scalar")
-        second_layer(0, "scalar")
+        second_layer(0, ("scalar", "scalar"), (nc.sync, nc.sync))
         rectify(2, 0, 4, "vector")
-        second_layer(1, "scalar")
-        second_layer(2, "vector")
+        second_layer(1, ("scalar",), (nc.scalar,))
+        second_layer(2, ("vector", "vector"), (nc.sync, nc.sync))

@@ -24,8 +24,8 @@ X_EARLY = 512
 FIRST_TILE = (
     (0, 256, "scalar"),
     (256, 256, "scalar"),
-    (512, 256, "scalar"),
-    (768, 128, "vector"),
+    (512, 256, "vector"),
+    (768, 128, "scalar"),
     (896, 128, "scalar"),
 )
 CHUNKS = ((256, 256), (128, 128), (0, 128))
@@ -39,7 +39,6 @@ def tile_picked_phpair_relu_p_kernel(
         lists = ctx.enter_context(tc.tile_pool(name="lists", bufs=1))
         keep = ctx.enter_context(tc.tile_pool(name="keep", bufs=1))
         turns = ctx.enter_context(tc.tile_pool(name="turns", bufs=1))
-        zpool = ctx.enter_context(tc.tile_pool(name="zpool", bufs=1))
         turns2 = ctx.enter_context(tc.tile_pool(name="turns2", bufs=1))
         psum = ctx.enter_context(tc.psum_pool(name="psum", bufs=8))
 
@@ -151,11 +150,11 @@ def tile_picked_phpair_relu_p_kernel(
         rights = [keep.tile([P, V], F32, name="right%d" % t, align_bytes=64) for t in (0, 1)]
         rights.append(keep.tile([P, V], F32, name="right2", align_bytes=64))
         rights.append(keep.tile([P, V], F32, name="right3", align_bytes=64))
-        diffs = turns.tile([P, PACK, V], F32, name="diffs", offset=0, align_bytes=64)
+        diffs = turns2.tile([P, PACK, V], F32, name="diffs", offset=0, align_bytes=64)
         z_bf = [
-            zpool.tile([P, PACK * 256], BF16, name="z_bf0", offset=0, align_bytes=64)[:],
+            keep.tile([P, PACK * 256], BF16, name="z_bf0", align_bytes=64)[:],
             keep.tile([P, PACK * 128], BF16, name="z_bf1", align_bytes=64)[:],
-            zpool.tile([P, PACK * 128], BF16, name="z_bf2", offset=0, align_bytes=64)[:],
+            diffs[:, 3, 256:V].bitcast(BF16),
         ]
 
         def fetch_right(t, lo, n):
@@ -170,10 +169,10 @@ def tile_picked_phpair_relu_p_kernel(
                 op=ALU.subtract,
             )
 
-        def rectify(c, t0, t1, engine):
-            lo, n = CHUNKS[c]
-            dst = z_bf[c].rearrange("p (a i t) -> p a t i", i=4, t=PACK)[:, :, t0:t1, :]
-            src = diffs[:, t0:t1, lo : lo + n].rearrange("p t (a i) -> p a t i", i=4)
+        def rectify(c, v0, v1, engine):
+            lo = CHUNKS[c][0]
+            dst = z_bf[c][:, PACK * v0 : PACK * v1].rearrange("p (a i t) -> p a t i", i=4, t=PACK)
+            src = diffs[:, :, lo + v0 : lo + v1].rearrange("p t (a i) -> p a t i", i=4)
             if engine == "vector":
                 nc.vector.tensor_scalar(out=dst, in0=src, scalar1=0.0, scalar2=None, op0=ALU.max)
             else:
@@ -237,9 +236,9 @@ def tile_picked_phpair_relu_p_kernel(
         for lo in (128, 0):
             fetch_right(3, lo, 128)
             fetch_left(3, lo, 128)
-        rectify(0, 0, 4, "scalar")
-        rectify(1, 0, 4, "scalar")
+        rectify(0, 0, 256, "scalar")
+        rectify(1, 0, 128, "scalar")
         second_layer(0, ("scalar", "scalar"), (nc.sync, nc.sync))
-        rectify(2, 0, 4, "vector")
-        second_layer(1, ("scalar",), (nc.scalar,))
-        second_layer(2, ("vector", "vector"), (nc.sync, nc.sync))
+        rectify(2, 0, 128, "vector")
+        second_layer(1, ("vector",), (nc.sync,))
+        second_layer(2, ("scalar", "vector"), (nc.scalar, nc.sync))

@@ -157,9 +157,12 @@ def tile_picked_phpair_relu_p_kernel(
             diffs[:, 3, 256:V].bitcast(BF16),
         ]
 
-        def fetch_right(t, lo, n):
-            offsets = right_sb[:, lo // LIST_ROWS : (lo + n) // LIST_ROWS]
-            nc.scalar.activation(out=rights[t][:, lo : lo + n], in_=h_sb[t][:].indirect(offsets), func=ACT.Copy)
+        def fetch_right(t, lo, n, engine="scalar"):
+            picked = h_sb[t][:].indirect(right_sb[:, lo // LIST_ROWS : (lo + n) // LIST_ROWS])
+            if engine == "vector":
+                nc.vector.tensor_copy(out=rights[t][:, lo : lo + n], in_=picked)
+            else:
+                nc.scalar.activation(out=rights[t][:, lo : lo + n], in_=picked, func=ACT.Copy)
 
         def fetch_left(t, lo, n):
             nc.vector.tensor_tensor(
@@ -193,11 +196,18 @@ def tile_picked_phpair_relu_p_kernel(
             )
 
 
-        def second_layer(c, engines, queues):
+        made = {}
+
+        def quantise_z(c):
             lo, n = CHUNKS[c]
             z_codes = keep.tile([P, n], U32, name="z_codes%d" % c, align_bytes=64)
             z_plane = keep.tile([P, n], U8, name="z_plane%d" % c, align_bytes=64)
             nc.vector.quantize_mx(out=z_codes[:].bitcast(FP8X4), scales=z_plane[:], in_=z_bf[c])
+            made[c] = (z_codes, z_plane)
+
+        def second_layer(c, engines, queues):
+            lo, n = CHUNKS[c]
+            z_codes, z_plane = made[c]
             for half in range(2):
                 if half == 0 or len(engines) == 2:
                     acc = psum.tile([P, 2, n], F32, name="acc")
@@ -233,12 +243,16 @@ def tile_picked_phpair_relu_p_kernel(
         for t in (1, 2):
             fetch_right(t, 0, 256)
             fetch_left(t, 0, 256)
+        rectify(0, 0, 64, "vector")
         for lo in (128, 0):
             fetch_right(3, lo, 128)
             fetch_left(3, lo, 128)
-        rectify(0, 0, 256, "scalar")
+        rectify(0, 64, 256, "scalar")
         rectify(1, 0, 128, "scalar")
+        quantise_z(0)
         second_layer(0, ("scalar", "scalar"), (nc.sync, nc.sync))
         rectify(2, 0, 128, "vector")
-        second_layer(1, ("vector",), (nc.sync,))
+        quantise_z(1)
+        second_layer(1, ("vector", "vector"), (nc.sync, nc.sync))
+        quantise_z(2)
         second_layer(2, ("scalar", "vector"), (nc.scalar, nc.sync))

@@ -40,7 +40,7 @@ def tile_picked_phpair_relu_p_kernel(
         keep = ctx.enter_context(tc.tile_pool(name="keep", bufs=1))
         turns = ctx.enter_context(tc.tile_pool(name="turns", bufs=1))
         turns2 = ctx.enter_context(tc.tile_pool(name="turns2", bufs=1))
-        psum = ctx.enter_context(tc.psum_pool(name="psum", bufs=8))
+        psum = ctx.enter_context(tc.psum_pool(name="psum", bufs=1))
 
         offs_sb = lists.tile([P, S // LIST_ROWS], U16, name="offs_sb")
         left_sb = lists.tile([P, V // LIST_ROWS], U16, name="left_sb")
@@ -115,8 +115,8 @@ def tile_picked_phpair_relu_p_kernel(
 
         h_sb = [keep.tile([P, S], F32, name="h_sb%d" % t, align_bytes=64) for t in range(PACK)]
 
-        def project(t, lo, width, engine):
-            acc = psum.tile([P, BANK], F32, name="acc")
+        def project(t, lo, width, engine, bank):
+            acc = psum.tile([P, BANK], F32, name="acc", tag="bank%d" % bank)
             nc.tensor.matmul_mx(
                 out=acc[:, 0:width],
                 lhsT=codes_w1(t, t + 1).bitcast(FP8X4),
@@ -144,25 +144,22 @@ def tile_picked_phpair_relu_p_kernel(
         round_w1(0, 4, 2, 4, "vector")
         quantise_w1(1, 2)
         quantise_w1(2, 4)
-        for lo, width, engine in FIRST_TILE:
-            project(0, lo, width, engine)
+        for bank, (lo, width, engine) in enumerate(FIRST_TILE):
+            project(0, lo, width, engine, bank)
 
         rights = [keep.tile([P, V], F32, name="right%d" % t, align_bytes=64) for t in (0, 1)]
         rights.append(keep.tile([P, V], F32, name="right2", align_bytes=64))
         rights.append(keep.tile([P, V], F32, name="right3", align_bytes=64))
-        diffs = turns2.tile([P, PACK, V], F32, name="diffs", offset=0, align_bytes=64)
+        diffs = turns.tile([P, PACK, V], F32, name="diffs", offset=0, align_bytes=64)
         z_bf = [
             keep.tile([P, PACK * 256], BF16, name="z_bf0", align_bytes=64)[:],
             keep.tile([P, PACK * 128], BF16, name="z_bf1", align_bytes=64)[:],
             diffs[:, 3, 256:V].bitcast(BF16),
         ]
 
-        def fetch_right(t, lo, n, engine="scalar"):
+        def fetch_right(t, lo, n):
             picked = h_sb[t][:].indirect(right_sb[:, lo // LIST_ROWS : (lo + n) // LIST_ROWS])
-            if engine == "vector":
-                nc.vector.tensor_copy(out=rights[t][:, lo : lo + n], in_=picked)
-            else:
-                nc.scalar.activation(out=rights[t][:, lo : lo + n], in_=picked, func=ACT.Copy)
+            nc.scalar.activation(out=rights[t][:, lo : lo + n], in_=picked, func=ACT.Copy)
 
         def fetch_left(t, lo, n):
             nc.vector.tensor_tensor(
@@ -182,9 +179,12 @@ def tile_picked_phpair_relu_p_kernel(
                 nc.scalar.activation(out=dst, in_=src, func=ACT.Relu)
 
         fetch_right(0, 0, V)
-        for t, engine in ((1, "vector"), (2, "scalar"), (3, "vector")):
-            for lo in range(0, S, BANK):
-                project(t, lo, BANK, engine)
+        project(1, 0, BANK, "vector", 5)
+        project(1, BANK, BANK, "vector", 6)
+        project(2, 0, BANK, "vector", 7)
+        project(2, BANK, BANK, "vector", 0)
+        project(3, 0, BANK, "scalar", 5)
+        project(3, BANK, BANK, "scalar", 6)
 
         w2_codes = keep.tile([P, 2 * N], U8, name="w2_codes", tag="words", align_bytes=64)
         w2_plane = w1_plane[:, H - N : H]
@@ -210,7 +210,7 @@ def tile_picked_phpair_relu_p_kernel(
             z_codes, z_plane = made[c]
             for half in range(2):
                 if half == 0 or len(engines) == 2:
-                    acc = psum.tile([P, 2, n], F32, name="acc")
+                    acc = psum.tile([P, 2, n], F32, name="acc", tag="bank%d" % (2 * c + half))
                 nc.tensor.matmul_mx(
                     out=acc[:, half, :],
                     lhsT=w2_codes[:, 2 * P * half : 2 * P * (half + 1)].bitcast(FP4X4),
@@ -243,11 +243,11 @@ def tile_picked_phpair_relu_p_kernel(
         for t in (1, 2):
             fetch_right(t, 0, 256)
             fetch_left(t, 0, 256)
-        rectify(0, 0, 64, "vector")
+        rectify(0, 0, 32, "vector")
         for lo in (128, 0):
             fetch_right(3, lo, 128)
             fetch_left(3, lo, 128)
-        rectify(0, 64, 256, "scalar")
+        rectify(0, 32, 256, "scalar")
         rectify(1, 0, 128, "scalar")
         quantise_z(0)
         second_layer(0, ("scalar", "scalar"), (nc.sync, nc.sync))

@@ -183,8 +183,8 @@ def tile_picked_phpair_relu_p_kernel(
         project(1, BANK, BANK, "vector", 6)
         project(2, 0, BANK, "vector", 7)
         project(2, BANK, BANK, "vector", 0)
-        project(3, 0, BANK, "scalar", 5)
-        project(3, BANK, BANK, "scalar", 6)
+        project(3, 0, BANK, "scalar", 4)
+        project(3, BANK, BANK, "scalar", 5)
 
         w2_codes = keep.tile([P, 2 * N], U8, name="w2_codes", tag="words", align_bytes=64)
         w2_plane = w1_plane[:, H - N : H]
@@ -243,11 +243,11 @@ def tile_picked_phpair_relu_p_kernel(
         for t in (1, 2):
             fetch_right(t, 0, 256)
             fetch_left(t, 0, 256)
-        rectify(0, 0, 32, "vector")
+        rectify(0, 0, 80, "vector")
         for lo in (128, 0):
             fetch_right(3, lo, 128)
             fetch_left(3, lo, 128)
-        rectify(0, 32, 256, "scalar")
+        rectify(0, 80, 256, "scalar")
         rectify(1, 0, 128, "scalar")
         quantise_z(0)
         second_layer(0, ("scalar", "scalar"), (nc.sync, nc.sync))

@@ -22,8 +22,7 @@ LIST_ROWS = 16
 BANK = 512
 X_EARLY = 512
 FIRST_TILE = (
-    (0, 256, "scalar"),
-    (256, 256, "scalar"),
+    (0, 512, "scalar"),
     (512, 256, "vector"),
     (768, 128, "scalar"),
     (896, 128, "scalar"),
@@ -182,9 +181,9 @@ def tile_picked_phpair_relu_p_kernel(
         project(1, 0, BANK, "vector", 5)
         project(1, BANK, BANK, "vector", 6)
         project(2, 0, BANK, "vector", 7)
-        project(2, BANK, BANK, "vector", 0)
-        project(3, 0, BANK, "scalar", 4)
-        project(3, BANK, BANK, "scalar", 5)
+        project(2, BANK, BANK, "scalar", 3)
+        project(3, 0, BANK, "vector", 5)
+        project(3, BANK, BANK, "scalar", 6)
 
         w2_codes = keep.tile([P, 2 * N], U8, name="w2_codes", tag="words", align_bytes=64)
         w2_plane = w1_plane[:, H - N : H]
@@ -243,11 +242,10 @@ def tile_picked_phpair_relu_p_kernel(
         for t in (1, 2):
             fetch_right(t, 0, 256)
             fetch_left(t, 0, 256)
-        rectify(0, 0, 80, "vector")
         for lo in (128, 0):
             fetch_right(3, lo, 128)
             fetch_left(3, lo, 128)
-        rectify(0, 80, 256, "scalar")
+        rectify(0, 0, 256, "scalar")
         rectify(1, 0, 128, "scalar")
         quantise_z(0)
         second_layer(0, ("scalar", "scalar"), (nc.sync, nc.sync))

from contextlib import ExitStack

import concourse.mybir as mybir

K, T, S, H, N, V = 512, 2048, 1024, 512, 256, 512
FLOPS = 2 * K * H * S + 2 * H * N * V

F32 = mybir.dt.float32
BF16 = mybir.dt.bfloat16
I32 = mybir.dt.int32
U32 = mybir.dt.uint32
U16 = mybir.dt.uint16
U8 = mybir.dt.uint8
FP8X4 = mybir.dt.float8_e4m3fn_x4
FP4X4 = mybir.dt.float4_e2m1fn_x4
ALU = mybir.AluOpType
ACT = mybir.ActivationFunctionType

P = 128
PACK = 4
LIST_ROWS = 16
BANK = 512
X_EARLY = 512
FIRST_TILE = (
    (0, 512, "scalar"),
    (512, 256, "vector"),
    (768, 128, "scalar"),
    (896, 128, "scalar"),
)
CHUNKS = ((256, 256), (128, 128), (0, 128))


def tile_picked_phpair_relu_p_kernel(
    tc, x_words, x_scales, w1, w2_words, w2_scales, offs, left, right, out
):
    nc = tc.nc
    with ExitStack() as ctx:
        lists = ctx.enter_context(tc.tile_pool(name="lists", bufs=1))
        keep = ctx.enter_context(tc.tile_pool(name="keep", bufs=1))
        turns = ctx.enter_context(tc.tile_pool(name="turns", bufs=1))
        turns2 = ctx.enter_context(tc.tile_pool(name="turns2", bufs=1))
        psum = ctx.enter_context(tc.psum_pool(name="psum", bufs=1))

        offs_sb = lists.tile([P, S // LIST_ROWS], U16, name="offs_sb")
        left_sb = lists.tile([P, V // LIST_ROWS], U16, name="left_sb")
        right_sb = lists.tile([P, V // LIST_ROWS], U16, name="right_sb")

        xs_table = keep.tile([P, T], U8, name="xs_table", align_bytes=64)
        xs_picked = keep.tile([P, S], U8, name="xs_picked", align_bytes=64)
        xs_plane = keep.tile([P, S], U8, name="xs_plane", align_bytes=64)
        xw_table = keep.tile([P, T], U32, name="xw_table", align_bytes=64)
        w1_raw = keep.tile([P, PACK * H], F32, name="w1_raw", align_bytes=64)
        staged = {
            0: turns.tile([P, H], BF16, name="staged0", offset=0, align_bytes=64),
            1: keep.tile([P, H], BF16, name="staged1", align_bytes=64),
            2: turns.tile([P, 2 * H], BF16, name="staged2", offset=H, align_bytes=64),
        }
        codes0 = keep.tile([P, P], U32, name="codes0", align_bytes=64)
        codes23 = turns2.tile([P, 2 * P], U32, name="codes23", offset=0, align_bytes=64)
        codes1 = turns.tile([P, P], U32, name="codes1", offset=0, align_bytes=64)
        w1_plane = keep.tile([P, H], U8, name="w1_plane", align_bytes=64)

        warm = keep.tile([P, 16], F32, name="warm", align_bytes=64)
        nc.vector.memset(xs_table[:].bitcast(I32), 0)
        nc.vector.memset(warm[:, 0:8], 0.0)
        nc.scalar.activation(out=warm[:, 8:16], in_=warm[:, 0:8], func=ACT.Relu)
        nc.vector.memset(xs_plane[:].bitcast(I32), 0)

        x_rows = x_words[0].rearrange("p c r -> p (c r)").bitcast(I32)
        nc.sync.dma_start(out=xw_table[:, 0:X_EARLY].bitcast(I32), in_=x_rows[:, 0:X_EARLY])
        nc.sync.dma_start(offs_sb[:], offs)
        nc.sync.dma_start(out=xs_table[0:P:8, :].bitcast(I32), in_=x_scales[0].bitcast(I32))
        nc.sync.dma_start(out=xw_table[:, X_EARLY:T].bitcast(I32), in_=x_rows[:, X_EARLY:T])
        w1_rows = w1.rearrange("(p j) c -> p (j c)", j=PACK)
        for lo in (0, 2 * H):
            nc.sync.dma_start(out=w1_raw[:, lo : lo + 2 * H], in_=w1_rows[:, lo : lo + 2 * H])
        nc.sync.dma_start(right_sb[:], right)
        nc.sync.dma_start(left_sb[:], left)

        nc.vector.tensor_copy(out=xs_picked[:], in_=xs_table[:].indirect(offs_sb[:]))
        for r in range(4):
            (nc.sync if r % 2 else nc.scalar).dma_start(
                out=xs_plane[r:P:32, :].bitcast(I32), in_=xs_picked[8 * r : P : 32, :].bitcast(I32)
            )

        xw_picked = keep.tile([P, S], U32, name="xw_picked", tag="words", align_bytes=64)
        nc.vector.tensor_copy(out=xw_picked[:], in_=xw_table[:].indirect(offs_sb[:]))

        def staged_w1(t0, t1):
            return staged[t0][:]

        def codes_w1(t0, t1):
            if t0 >= 2:
                return codes23[:, P * (t0 - 2) : P * (t1 - 2)]
            return codes1[:] if t0 == 1 else codes0[:]

        def round_w1(j0, j1, t0, t1, engine):
            rows = w1_raw[:, H * j0 : H * j1].rearrange("p (j m t) -> p m t j", j=j1 - j0, t=PACK)
            words = staged_w1(t0, t1).rearrange("p (t m j) -> p m t j", t=t1 - t0, j=PACK)
            dst, src = words[:, :, :, j0:j1], rows[:, :, t0:t1, :]
            if engine == "vector":
                nc.vector.tensor_copy(out=dst, in_=src)
            elif engine == "gpsimd":
                nc.gpsimd.tensor_scalar(out=dst, in0=src, scalar1=1.0, scalar2=0.0, op0=ALU.mult, op1=ALU.add)
            else:
                nc.scalar.activation(out=dst, in_=src, func=ACT.Copy)

        def quantise_w1(t0, t1):
            nc.vector.quantize_mx(
                out=codes_w1(t0, t1).bitcast(FP8X4),
                scales=w1_plane[:, P * t0 : P * t1],
                in_=staged_w1(t0, t1),
            )

        h_sb = [keep.tile([P, S], F32, name="h_sb%d" % t, align_bytes=64) for t in range(PACK)]

        def project(t, lo, width, engine, bank):
            acc = psum.tile([P, BANK], F32, name="acc", tag="bank%d" % bank)
            nc.tensor.matmul_mx(
                out=acc[:, 0:width],
                lhsT=codes_w1(t, t + 1).bitcast(FP8X4),
                lhsT_scale=w1_plane[:, P * t : P * (t + 1)],
                rhs=xw_picked[:, lo : lo + width].bitcast(FP8X4),
                rhs_scale=xs_plane[:, lo : lo + width],
                start=True,
                stop=True,
            )
            if engine == "vector":
                nc.vector.tensor_copy(out=h_sb[t][:, lo : lo + width], in_=acc[:, 0:width])
            else:
                nc.scalar.copy(out=h_sb[t][:, lo : lo + width], in_=acc[:, 0:width])

        round_w1(0, 2, 0, 1, "scalar")
        round_w1(0, 2, 1, 2, "gpsimd")
        rows = w1_raw[:, 2 * H : 4 * H].rearrange("p (j m t) -> p m t j", j=2, t=PACK)[:, :, 0, :]
        words = staged_w1(0, 1).rearrange("p (m j) -> p m j", j=PACK)[:, :, 2:4]
        nc.scalar.activation(out=words[:, 0:64, :], in_=rows[:, 0:64, :], func=ACT.Copy)
        nc.gpsimd.tensor_scalar(
            out=words[:, 64:P, :], in0=rows[:, 64:P, :], scalar1=1.0, scalar2=0.0, op0=ALU.mult, op1=ALU.add
        )
        quantise_w1(0, 1)
        round_w1(2, 4, 1, 2, "scalar")
        round_w1(0, 4, 2, 4, "vector")
        quantise_w1(1, 2)
        quantise_w1(2, 4)
        for bank, (lo, width, engine) in enumerate(FIRST_TILE):
            project(0, lo, width, engine, bank)

        rights = [keep.tile([P, V], F32, name="right%d" % t, align_bytes=64) for t in (0, 1)]
        rights.append(keep.tile([P, V], F32, name="right2", align_bytes=64))
        rights.append(keep.tile([P, V], F32, name="right3", align_bytes=64))
        diffs = turns.tile([P, PACK, V], F32, name="diffs", offset=0, align_bytes=64)
        z_bf = [
            keep.tile([P, PACK * 256], BF16, name="z_bf0", align_bytes=64)[:],
            keep.tile([P, PACK * 128], BF16, name="z_bf1", align_bytes=64)[:],
            diffs[:, 3, 256:V].bitcast(BF16),
        ]

        def fetch_right(t, lo, n):
            picked = h_sb[t][:].indirect(right_sb[:, lo // LIST_ROWS : (lo + n) // LIST_ROWS])
            nc.scalar.activation(out=rights[t][:, lo : lo + n], in_=picked, func=ACT.Copy)

        def fetch_left(t, lo, n):
            nc.vector.tensor_tensor(
                out=diffs[:, t, lo : lo + n],
                in0=h_sb[t][:].indirect(left_sb[:, lo // LIST_ROWS : (lo + n) // LIST_ROWS]),
                in1=rights[t][:, lo : lo + n],
                op=ALU.subtract,
            )

        def rectify(c, v0, v1, engine):
            lo = CHUNKS[c][0]
            dst = z_bf[c][:, PACK * v0 : PACK * v1].rearrange("p (a i t) -> p a t i", i=4, t=PACK)
            src = diffs[:, :, lo + v0 : lo + v1].rearrange("p t (a i) -> p a t i", i=4)
            if engine == "vector":
                nc.vector.tensor_scalar(out=dst, in0=src, scalar1=0.0, scalar2=None, op0=ALU.max)
            else:
                nc.scalar.activation(out=dst, in_=src, func=ACT.Relu)

        fetch_right(0, 0, V)
        project(1, 0, BANK, "vector", 5)
        project(1, BANK, BANK, "vector", 6)
        project(2, 0, BANK, "vector", 7)
        project(2, BANK, BANK, "scalar", 3)
        project(3, 0, BANK, "vector", 5)
        project(3, BANK, BANK, "scalar", 6)

        w2_codes = keep.tile([P, 2 * N], U8, name="w2_codes", tag="words", align_bytes=64)
        w2_plane = w1_plane[:, H - N : H]
        nc.sync.dma_start(out=w2_codes[:].bitcast(I32), in_=w2_words[0].bitcast(I32))
        for q in range(4):
            nc.sync.dma_start(
                out=w2_plane[32 * q : 32 * q + 4, :].bitcast(I32),
                in_=w2_scales[0, 4 * q : 4 * q + 4, :].bitcast(I32),
            )


        made = {}

        def quantise_z(c):
            lo, n = CHUNKS[c]
            z_codes = keep.tile([P, n], U32, name="z_codes%d" % c, align_bytes=64)
            z_plane = keep.tile([P, n], U8, name="z_plane%d" % c, align_bytes=64)
            nc.vector.quantize_mx(out=z_codes[:].bitcast(FP8X4), scales=z_plane[:], in_=z_bf[c])
            made[c] = (z_codes, z_plane)

        def second_layer(c, engines, queues):
            lo, n = CHUNKS[c]
            z_codes, z_plane = made[c]
            for half in range(2):
                if half == 0 or len(engines) == 2:
                    acc = psum.tile([P, 2, n], F32, name="acc", tag="bank%d" % (2 * c + half))
                nc.tensor.matmul_mx(
                    out=acc[:, half, :],
                    lhsT=w2_codes[:, 2 * P * half : 2 * P * (half + 1)].bitcast(FP4X4),
                    lhsT_scale=w2_plane[:, P * half : P * (half + 1)],
                    rhs=z_codes[:].bitcast(FP8X4),
                    rhs_scale=z_plane[:],
                    start=True,
                    stop=True,
                )
                if len(engines) == 2:
                    leave(c, half, half + 1, acc, engines[half], queues[half])
            if len(engines) == 1:
                leave(c, 0, 2, acc, engines[0], queues[0])

        def leave(c, h0, h1, acc, engine, queue):
            lo, n = CHUNKS[c]
            result = keep.tile([P, h1 - h0, n], F32, name="result%d_%d" % (c, h0), align_bytes=64)
            if engine == "vector":
                nc.vector.tensor_copy(out=result[:], in_=acc[:, h0:h1, :])
            else:
                nc.scalar.copy(out=result[:], in_=acc[:, h0:h1, :])
            queue.dma_start(
                out=out[P * h0 : P * h1, lo : lo + n].rearrange("(a p) v -> p a v", p=P), in_=result[:]
            )

        fetch_left(0, 0, V)
        for t in (1, 2, 3):
            fetch_right(t, 256, 256)
            fetch_left(t, 256, 256)
        for t in (1, 2):
            fetch_right(t, 0, 256)
            fetch_left(t, 0, 256)
        for lo in (128, 0):
            fetch_right(3, lo, 128)
            fetch_left(3, lo, 128)
        rectify(0, 0, 256, "scalar")
        rectify(1, 0, 128, "scalar")
        quantise_z(0)
        second_layer(0, ("scalar", "scalar"), (nc.sync, nc.sync))
        rectify(2, 0, 128, "vector")
        quantise_z(1)
        second_layer(1, ("vector", "vector"), (nc.sync, nc.sync))
        quantise_z(2)
        second_layer(2, ("scalar", "vector"), (nc.scalar, nc.sync))
